import numpy as np
import ml_dtypes


def mxq(x, axis, fmt="e4m3"):
    dtype, down = {"e4m3": (ml_dtypes.float8_e4m3fn, 7), "e5m2": (ml_dtypes.float8_e5m2, 14)}[fmt]
    v = np.moveaxis(np.asarray(x, np.float32).astype(ml_dtypes.bfloat16).astype(np.float64), axis, -1)
    blocks = v.reshape(v.shape[:-1] + (-1, 32))
    amax = np.abs(blocks).max(-1, keepdims=True)
    byte = np.maximum(np.where(amax > 0, np.frexp(amax)[1] - 1 + 127, 0) - down, 1)
    scale = np.exp2(byte - 127.0)
    codes = (blocks / scale).astype(np.float32).astype(dtype).astype(np.float64)
    return np.moveaxis((codes * scale).reshape(v.shape), -1, axis)


WIDE = False


def mx_kscale(k):
    if not WIDE:
        return np.ones(k)
    levels = np.array([30, -30])
    if k % 512:
        return np.exp2(np.random.permutation(np.resize(levels, k // 32))).repeat(32)
    a = np.empty((k // 512, 16))
    for p in range(k // 512):
        a[p, :8] = np.random.permutation(np.resize(levels, 8))
        for g in range(8):
            far = levels[np.abs(levels - a[p, g]) >= 10]
            a[p, g + 8] = far[np.random.randint(len(far))]
    return np.exp2(a.ravel()).repeat(32)


def f64(x):
    return np.asarray(x).astype(np.float64)


def striped(idx):
    return np.tile(idx.reshape(-1, 16).T, (8, 1)).astype(np.uint16)


def unstriped(offs):
    return offs[:16].T.reshape(-1).astype(np.int64)


def bf(x):
    return np.asarray(x, np.float32).astype(ml_dtypes.bfloat16)


E2M1 = np.array([0.0, 0.5, 1.0, 1.5, 2.0, 3.0, 4.0, 6.0, -0.0, -0.5, -1.0, -1.5, -2.0, -3.0, -4.0, -6.0])


def pack_weight(w, fmt):
    k, n = w.shape
    w = f64(bf(w)).reshape(k // 32, 32, n)
    amax = np.abs(w).max(1)
    if fmt in ("e4m3", "e5m2"):
        byte = np.frexp(amax)[1] - 1 + 127 - (7 if fmt == "e4m3" else 14)
    else:
        mant, ex = np.frexp(amax / 6.0)
        byte = np.where(mant > 0.5, ex, ex - 1) + 127
    byte = np.clip(np.where(amax > 0, byte, 1), 1, 254)
    scaled = (w * np.exp2(127.0 - byte)[:, None, :]).reshape(k, n).astype(np.float32)
    by_word = np.ascontiguousarray(scaled.reshape(k // 512, 128, 4, n).transpose(0, 1, 3, 2))
    if fmt in ("e4m3", "e5m2"):
        words = by_word.astype(ml_dtypes.float8_e4m3fn if fmt == "e4m3" else ml_dtypes.float8_e5m2).view(np.uint8)
    else:
        c = by_word.astype(ml_dtypes.float4_e2m1fn).view(np.uint8) & 0xF
        words = c[..., 0::2] | (c[..., 1::2] << 4)
    return np.ascontiguousarray(words), np.ascontiguousarray(byte.astype(np.uint8).reshape(k // 512, 16, n))


def unpack_weight(words, scales, fmt):
    g, p, n, _ = words.shape
    if fmt in ("e4m3", "e5m2"):
        vals = np.ascontiguousarray(words).view(ml_dtypes.float8_e4m3fn if fmt == "e4m3" else ml_dtypes.float8_e5m2).astype(np.float64)
    else:
        nib = np.empty((g, p, n, 4), np.uint8)
        nib[..., 0::2] = words & 0xF
        nib[..., 1::2] = words >> 4
        vals = E2M1[nib]
    vals = vals * np.repeat(np.exp2(scales.astype(np.float64) - 127.0), 8, axis=1)[..., None]
    return vals.transpose(0, 1, 3, 2).reshape(g * 512, n)


K, T, S, T2 = 1024, 2048, 512, 1024

def setup_inputs():
    n = np.random.standard_normal
    s = mx_kscale(K)[:, None]
    v = n((K, T)) * np.exp(1.0 * n((1, T))) * s
    tab_words, tab_scales = pack_weight(v, "e5m2")
    wa = (n((K, K)) / np.sqrt(K) / s * s.T).astype(np.float32)
    wb_words, wb_scales = pack_weight(n((K, K)) / np.sqrt(K) / s * s.T, "e4m3")
    return {
        "tab_words": tab_words, "tab_scales": tab_scales,
        "wa": wa,
        "wb_words": wb_words, "wb_scales": wb_scales,
        "sT": (1.0 / (1.0 + np.exp(-n((K, T))))).astype(np.float32),
        "gain": (np.exp(1.0 + 0.3 * n(K)) / s[:, 0]).astype(np.float32),
        "wgo": np.exp(0.3 * n((128, S))).astype(np.float32),
        "offs": striped(np.random.permutation(T)[:S]),
        "offs2": striped(np.random.permutation(T2)[:S]),
    }

def reference(tab_words, tab_scales, wa, wb_words, wb_scales, sT, gain, wgo, offs, offs2):
    v = unpack_weight(tab_words, tab_scales, "e5m2")[:, unstriped(offs)]
    x = f64(sT)[:, unstriped(offs)]
    d = x * (1.0 - x)
    aq = mxq(f64(wa), 0, "e4m3")
    bq = unpack_weight(wb_words, wb_scales, "e4m3")
    hb = mxq(d * (bq.T @ v), 0, "e4m3")
    ha = mxq(d * (aq.T @ v), 0, "e4m3")
    comm = (aq.T @ hb) - (bq.T @ ha)
    y = f64(gain)[:, None] * comm
    out = np.zeros((K, T2))
    out[:, unstriped(offs2)] = np.tile(f64(wgo), (K // 128, 1)) * y
    return out

@@ -1,0 +1,309 @@
+from contextlib import ExitStack
+
+import concourse.mybir as mybir
+
+K, T, S, T2 = 1024, 2048, 512, 1024
+FLOPS = 4 * 2 * K * K * S
+
+F32 = mybir.dt.float32
+BF16 = mybir.dt.bfloat16
+I32 = mybir.dt.int32
+U32 = mybir.dt.uint32
+U16 = mybir.dt.uint16
+U8 = mybir.dt.uint8
+E4M3 = mybir.dt.float8_e4m3fn_x4
+E5M2 = mybir.dt.float8_e5m2_x4
+MULT = mybir.AluOpType.mult
+SUB = mybir.AluOpType.subtract
+COPY = mybir.ActivationFunctionType.Copy
+
+P = 128
+PACK = 4
+SPAN = P * PACK
+PASSES = K // SPAN
+HALF = S // 2
+WINDOWS = 3
+
+
+def tile_list_slope_weighted_commutator_kernel(
+    tc, tab_words, tab_scales, wa, wb_words, wb_scales, sT, gain, wgo, offs, offs2, out
+):
+    nc = tc.nc
+    with ExitStack() as ctx:
+        keep = ctx.enter_context(tc.tile_pool(name="keep", bufs=1))
+        rows = ctx.enter_context(tc.tile_pool(name="rows", bufs=6))
+        cast = ctx.enter_context(tc.tile_pool(name="cast", bufs=2))
+        res = ctx.enter_context(tc.tile_pool(name="res", bufs=3))
+        psum = ctx.enter_context(tc.psum_pool(name="psum", bufs=1))
+
+        def kept(name, width, dtype):
+            return keep.tile([P, width], dtype, name=name, align_bytes=64)
+
+        idx = keep.tile([P, S // 16], U16, name="idx")
+        idx2 = keep.tile([P, S // 16], U16, name="idx2")
+        tab_w = [kept("tab_w%d" % a, T, I32) for a in range(PASSES)]
+        tab_s = kept("tab_s", PASSES * T, U8)
+        v_w = [kept("v_w%d" % a, S, U32) for a in range(PASSES)]
+        v_s = [kept("v_s%d" % a, S, U8) for a in range(PASSES)]
+        wb_raw_w = kept("wb_raw_w", PASSES * K, I32)
+        wb_raw_s = kept("wb_raw_s", PASSES * K, U8)
+        wb_w = kept("wb_w", PASSES * K, I32)
+        wb_s = kept("wb_s", PASSES * K, U8)
+        blocks = [(a, b) for b in range(PASSES) for a in range(PASSES)]
+        wa_raw = {ab: kept("wa_raw%d%d" % ab, PACK * SPAN, F32) for ab in blocks}
+        wa_w = {ab: kept("wa_w%d%d" % ab, SPAN, U32) for ab in blocks}
+        wa_s = {ab: kept("wa_s%d%d" % ab, SPAN, U8) for ab in blocks}
+        slices = [(b, t) for b in range(PASSES) for t in range(PACK)]
+        nd = {bt: kept("nd%d%d" % bt, S, F32) for bt in slices}
+        prods = [(w, b) for b in range(PASSES) for w in "ba"]
+        planes = {wb_: kept("planes%s%d" % wb_, PACK * S, BF16) for wb_ in prods}
+        woven = {wb_: kept("woven%s%d" % wb_, PACK * S, BF16) for wb_ in prods}
+        h_w = {wb_: kept("h_w%s%d" % wb_, S, U32) for wb_ in prods}
+        h_s = {wb_: kept("h_s%s%d" % wb_, S, U8) for wb_ in prods}
+        wgo_t = kept("wgo_t", PACK * S, F32)
+        gain_t = kept("gain_t", PASSES * PACK, F32)
+        windows = [kept("window%d" % i, T2, F32) for i in range(WINDOWS)]
+
+        nc.gpsimd.memset(tab_s[:].bitcast(I32), 0)
+        nc.vector.memset(wb_raw_s[:].bitcast(I32), 0)
+        for window in windows:
+            nc.vector.memset(window[:], 0.0)
+
+        def load_scales(src, dst):
+            for q in range(4):
+                nc.sync.dma_start(
+                    out=dst[32 * q : 32 * q + 4, :].bitcast(I32).rearrange("p (a c) -> p a c", a=PASSES),
+                    in_=src[:, 4 * q : 4 * q + 4, :].rearrange("a r c -> r a c").bitcast(I32),
+                )
+
+        s_rows = {}
+
+        def load_rows(b, t):
+            s_rows[b, t] = rows.tile([P, T], F32, name="s_rows")
+            nc.sync.dma_start(out=s_rows[b, t][:], in_=sT.rearrange("(b p t) c -> b t p c", p=P, t=PACK)[b, t])
+
+        def load_wa(a, b):
+            nc.sync.dma_start(
+                out=wa_raw[a, b][:].rearrange("p (i c) -> p i c", i=PACK),
+                in_=wa[a * SPAN : (a + 1) * SPAN, b * SPAN : (b + 1) * SPAN].rearrange("(p i) c -> p i c", i=PACK),
+            )
+
+        nc.sync.dma_start(idx[:], offs)
+        nc.sync.dma_start(out=tab_w[0][:], in_=tab_words[0].rearrange("p c i -> p (c i)").bitcast(I32))
+        load_scales(tab_scales, tab_s)
+        nc.sync.dma_start(out=tab_w[1][:], in_=tab_words[1].rearrange("p c i -> p (c i)").bitcast(I32))
+        nc.sync.dma_start(
+            out=wb_raw_w[:].rearrange("p (a c) -> p a c", a=PASSES),
+            in_=wb_words.rearrange("a p c i -> p a (c i)").bitcast(I32),
+        )
+        load_scales(wb_scales, wb_raw_s)
+
+        def gather_table(a):
+            nc.vector.tensor_copy(v_w[a][:], tab_w[a][:].bitcast(U32).indirect(idx[:]))
+            nc.vector.tensor_copy(v_s[a][:], tab_s[:, a * T : (a + 1) * T].indirect(idx[:]))
+
+        def order_wb():
+            for src, dst in ((wb_raw_w, wb_w), (wb_raw_s, wb_s)):
+                nc.vector.tensor_copy(
+                    dst[:].rearrange("p (g t m) -> p g m t", t=PACK, m=P),
+                    src[:].rearrange("p (g m t) -> p g m t", t=PACK, m=P),
+                )
+
+        wa_bf = {}
+
+        def cast_wa(a, b):
+            wa_bf[a, b] = cast.tile([P, PACK * SPAN], BF16, name="wa_bf", align_bytes=64)
+            nc.scalar.activation(
+                wa_bf[a, b][:].rearrange("p (t m i) -> p m i t", t=PACK, i=PACK),
+                wa_raw[a, b][:].rearrange("p (i m t) -> p m i t", t=PACK, i=PACK),
+                COPY,
+            )
+
+        def quantise_wa(a, b):
+            nc.vector.quantize_mx(out=wa_w[a, b][:].bitcast(E4M3), scales=wa_s[a, b][:], in_=wa_bf[a, b][:])
+
+        def weights(w, a, b, t):
+            if w == "a":
+                cols = slice(t * P, (t + 1) * P)
+                return wa_w[a, b][:, cols].bitcast(E4M3), wa_s[a, b][:, cols]
+            c0 = a * K + b * SPAN + t * P
+            return wb_w[:, c0 : c0 + P].bitcast(E4M3), wb_s[:, c0 : c0 + P]
+
+        first = {}
+
+        def stage1(w, b, t):
+            first[w, b, t] = psum.tile([P, S], F32, name="first", tag="bank%s%d" % (w, t))
+            for a in range(PASSES):
+                codes, scales = weights(w, a, b, t)
+                nc.tensor.matmul_mx(
+                    out=first[w, b, t][:],
+                    lhsT=codes,
+                    lhsT_scale=scales,
+                    rhs=v_w[a][:].bitcast(E5M2),
+                    rhs_scale=v_s[a][:],
+                    start=(a == 0),
+                    stop=(a == PASSES - 1),
+                )
+
+        picked = {}
+
+        def gather_rows(b, t, j0, j1):
+            picked[b, t, j0] = res.tile([P, j1 - j0], F32, name="picked", tag="picked")
+            nc.vector.tensor_copy(picked[b, t, j0][:], s_rows[b, t][:].indirect(idx[:, j0 // 16 : j1 // 16]))
+
+        def slope(b, t, j0, j1):
+            x = picked[b, t, j0][:]
+            nc.vector.scalar_tensor_tensor(nd[b, t][:, j0:j1], x, 1.0, x, SUB, MULT)
+
+        def weigh(w, b, t, j0, j1):
+            h0, h1 = j0 // HALF, j1 // HALF
+            dst = planes[w, b][:].rearrange("p (h t j) -> p h t j", t=PACK, j=HALF)[:, h0:h1, t, :]
+            acc = first[w, b, t][:, j0:j1].rearrange("p (h j) -> p h j", j=HALF)
+            slp = nd[b, t][:, j0:j1].rearrange("p (h j) -> p h j", j=HALF)
+            nc.vector.scalar_tensor_tensor(dst, acc, -1.0 if w == "b" else 1.0, slp, MULT, MULT)
+
+        def weave(engine_copy, w, b, j0, j1):
+            cols = slice(PACK * j0, PACK * j1)
+            engine_copy(
+                woven[w, b][:, cols].rearrange("p (h c i t) -> p h c t i", t=PACK, i=4, c=HALF // 4),
+                planes[w, b][:, cols].rearrange("p (h t c i) -> p h c t i", t=PACK, i=4, c=HALF // 4),
+            )
+
+        def quantise_h(w, b, j0, j1):
+            nc.vector.quantize_mx(
+                out=h_w[w, b][:, j0:j1].bitcast(E4M3),
+                scales=h_s[w, b][:, j0:j1],
+                in_=woven[w, b][:, PACK * j0 : PACK * j1],
+            )
+
+        banks = ["bank%s%d" % (w, t) for t in range(PACK) for w in "ba"]
+        y = {}
+
+        def stage2(unit, b, t, j0, j1):
+            acc = psum.tile([P, j1 - j0], F32, name="second", tag=banks[unit % len(banks)])
+            for n, (w, r) in enumerate(prods):
+                codes, scales = weights("a" if w == "b" else "b", r, b, t)
+                nc.tensor.matmul_mx(
+                    out=acc[:],
+                    lhsT=codes,
+                    lhsT_scale=scales,
+                    rhs=h_w[w, r][:, j0:j1].bitcast(E4M3),
+                    rhs_scale=h_s[w, r][:, j0:j1],
+                    start=(n == 0),
+                    stop=(n == len(prods) - 1),
+                )
+            y[b, t, j0] = res.tile([P, j1 - j0], F32, name="y", tag="y")
+            c = b * PACK + t
+            nc.scalar.activation(y[b, t, j0][:], acc[:], COPY, scale=gain_t[:, c : c + 1])
+
+        def place(n, b, t, j0, j1):
+            nc.vector.tensor_tensor(
+                windows[n % WINDOWS][:].indirect(idx2[:, j0 // 16 : j1 // 16]),
+                y[b, t, j0][:],
+                wgo_t[:, t * S + j0 : t * S + j1],
+                MULT,
+            )
+
+        def store(n, b, t):
+            nc.sync.dma_start(
+                out=out.rearrange("(b p t) c -> b t p c", p=P, t=PACK)[b, t], in_=windows[n % WINDOWS][:]
+            )
+
+        def slice_step(b, t):
+            gather_rows(b, t, 0, S)
+            slope(b, t, 0, S)
+
+        load_wa(0, 0)
+        load_rows(0, 0)
+        load_wa(1, 0)
+        load_rows(0, 1)
+        load_rows(0, 2)
+        load_rows(0, 3)
+        load_wa(0, 1)
+        load_rows(1, 0)
+        load_wa(1, 1)
+        load_rows(1, 1)
+
+        gather_table(0)
+        gather_table(1)
+        order_wb()
+        cast_wa(0, 0)
+        cast_wa(1, 0)
+        for t in range(PACK):
+            stage1("b", 0, t)
+        slice_step(0, 0)
+        load_rows(1, 2)
+        quantise_wa(0, 0)
+        weigh("b", 0, 0, 0, S)
+        slice_step(0, 1)
+        load_rows(1, 3)
+        nc.sync.dma_start(idx2[:], offs2)
+        nc.sync.dma_start(
+            out=gain_t[:].rearrange("p (b t) -> p b t", t=PACK),
+            in_=gain.rearrange("(b p t) -> p b t", p=P, t=PACK),
+        )
+        for q in range(4):
+            nc.sync.dma_start(out=wgo_t[32 * q : 32 * (q + 1), :], in_=wgo.rearrange("(p t) j -> p (t j)", t=PACK))
+        quantise_wa(1, 0)
+        weigh("b", 0, 1, 0, S)
+        for t in range(PACK):
+            stage1("a", 0, t)
+        slice_step(0, 2)
+        weigh("a", 0, 0, 0, S)
+        weigh("b", 0, 2, 0, S)
+        weigh("a", 0, 1, 0, S)
+        weigh("a", 0, 2, 0, S)
+        slice_step(0, 3)
+        cast_wa(0, 1)
+        weigh("b", 0, 3, 0, S)
+        weigh("a", 0, 3, 0, S)
+        weave(nc.scalar.copy, "b", 0, 0, S)
+        for t in range(PACK):
+            stage1("b", 1, t)
+        slice_step(1, 0)
+        cast_wa(1, 1)
+        quantise_wa(0, 1)
+        weigh("b", 1, 0, 0, S)
+        quantise_h("b", 0, 0, S)
+        weave(nc.scalar.copy, "a", 0, 0, S)
+        slice_step(1, 1)
+        quantise_wa(1, 1)
+        weigh("b", 1, 1, 0, S)
+        for t in range(PACK):
+            stage1("a", 1, t)
+        slice_step(1, 2)
+        weigh("a", 1, 0, 0, S)
+        weigh("b", 1, 2, 0, S)
+        weigh("a", 1, 1, 0, S)
+        weigh("a", 1, 2, 0, S)
+        quantise_h("a", 0, 0, S)
+
+        halves = [(0, HALF), (HALF, S)]
+        for j0, j1 in halves:
+            gather_rows(1, 3, j0, j1)
+        for j0, j1 in halves:
+            slope(1, 3, j0, j1)
+        for j0, j1 in halves:
+            weigh("b", 1, 3, j0, j1)
+            weigh("a", 1, 3, j0, j1)
+        weave(nc.scalar.copy, "b", 1, 0, HALF)
+        weave(nc.scalar.copy, "b", 1, HALF, S)
+        weave(nc.vector.tensor_copy, "a", 1, 0, HALF)
+        quantise_h("b", 1, 0, HALF)
+        quantise_h("a", 1, 0, HALF)
+        weave(nc.vector.tensor_copy, "a", 1, HALF, S)
+        order = [(b, t) for t in range(PACK) for b in range(PASSES)]
+        stage2(0, *order[0], 0, HALF)
+        stage2(1, *order[1], 0, HALF)
+        place(0, *order[0], 0, HALF)
+        quantise_h("b", 1, HALF, S)
+        quantise_h("a", 1, HALF, S)
+        place(1, *order[1], 0, HALF)
+        for n in range(2):
+            stage2(2 + n, *order[n], HALF, S)
+            place(n, *order[n], HALF, S)
+            store(n, *order[n])
+        for n in range(2, len(order)):
+            stage2(2 + n, *order[n], 0, S)
+            place(n, *order[n], 0, S)
+            store(n, *order[n])

@@ -31,7 +31,7 @@ def tile_list_slope_weighted_commutator_kernel(
     nc = tc.nc
     with ExitStack() as ctx:
         keep = ctx.enter_context(tc.tile_pool(name="keep", bufs=1))
-        rows = ctx.enter_context(tc.tile_pool(name="rows", bufs=6))
+        stage = ctx.enter_context(tc.tile_pool(name="stage", bufs=12))
         cast = ctx.enter_context(tc.tile_pool(name="cast", bufs=2))
         res = ctx.enter_context(tc.tile_pool(name="res", bufs=3))
         psum = ctx.enter_context(tc.psum_pool(name="psum", bufs=1))
@@ -41,16 +41,13 @@ def tile_list_slope_weighted_commutator_kernel(
 
         idx = keep.tile([P, S // 16], U16, name="idx")
         idx2 = keep.tile([P, S // 16], U16, name="idx2")
-        tab_w = [kept("tab_w%d" % a, T, I32) for a in range(PASSES)]
         tab_s = kept("tab_s", PASSES * T, U8)
         v_w = [kept("v_w%d" % a, S, U32) for a in range(PASSES)]
         v_s = [kept("v_s%d" % a, S, U8) for a in range(PASSES)]
-        wb_raw_w = kept("wb_raw_w", PASSES * K, I32)
         wb_raw_s = kept("wb_raw_s", PASSES * K, U8)
-        wb_w = kept("wb_w", PASSES * K, I32)
-        wb_s = kept("wb_s", PASSES * K, U8)
+        wb_w = [kept("wb_w%d" % a, K, I32) for a in range(PASSES)]
+        wb_s = [kept("wb_s%d" % a, K, U8) for a in range(PASSES)]
         blocks = [(a, b) for b in range(PASSES) for a in range(PASSES)]
-        wa_raw = {ab: kept("wa_raw%d%d" % ab, PACK * SPAN, F32) for ab in blocks}
         wa_w = {ab: kept("wa_w%d%d" % ab, SPAN, U32) for ab in blocks}
         wa_s = {ab: kept("wa_s%d%d" % ab, SPAN, U8) for ab in blocks}
         slices = [(b, t) for b in range(PASSES) for t in range(PACK)]
@@ -60,11 +57,11 @@ def tile_list_slope_weighted_commutator_kernel(
         woven = {wb_: kept("woven%s%d" % wb_, PACK * S, BF16) for wb_ in prods}
         h_w = {wb_: kept("h_w%s%d" % wb_, S, U32) for wb_ in prods}
         h_s = {wb_: kept("h_s%s%d" % wb_, S, U8) for wb_ in prods}
-        wgo_t = kept("wgo_t", PACK * S, F32)
         gain_t = kept("gain_t", PASSES * PACK, F32)
         windows = [kept("window%d" % i, T2, F32) for i in range(WINDOWS)]
 
-        nc.gpsimd.memset(tab_s[:].bitcast(I32), 0)
+        nc.gpsimd.memset(tab_s[:, :T].bitcast(I32), 0)
+        nc.vector.memset(tab_s[:, T:].bitcast(I32), 0)
         nc.vector.memset(wb_raw_s[:].bitcast(I32), 0)
         for window in windows:
             nc.vector.memset(window[:], 0.0)
@@ -76,38 +73,60 @@ def tile_list_slope_weighted_commutator_kernel(
                     in_=src[:, 4 * q : 4 * q + 4, :].rearrange("a r c -> r a c").bitcast(I32),
                 )
 
-        s_rows = {}
+        def staged(name, dtype):
+            return stage.tile([P, T], dtype, name=name, tag="staged", align_bytes=64)
+
+        s_rows, wa_raw, tab_w = {}, {}, {}
 
         def load_rows(b, t):
-            s_rows[b, t] = rows.tile([P, T], F32, name="s_rows")
+            s_rows[b, t] = staged("s_rows", F32)
             nc.sync.dma_start(out=s_rows[b, t][:], in_=sT.rearrange("(b p t) c -> b t p c", p=P, t=PACK)[b, t])
 
         def load_wa(a, b):
+            wa_raw[a, b] = staged("wa_raw", F32)
             nc.sync.dma_start(
                 out=wa_raw[a, b][:].rearrange("p (i c) -> p i c", i=PACK),
                 in_=wa[a * SPAN : (a + 1) * SPAN, b * SPAN : (b + 1) * SPAN].rearrange("(p i) c -> p i c", i=PACK),
             )
 
-        nc.sync.dma_start(idx[:], offs)
-        nc.sync.dma_start(out=tab_w[0][:], in_=tab_words[0].rearrange("p c i -> p (c i)").bitcast(I32))
-        load_scales(tab_scales, tab_s)
-        nc.sync.dma_start(out=tab_w[1][:], in_=tab_words[1].rearrange("p c i -> p (c i)").bitcast(I32))
-        nc.sync.dma_start(
-            out=wb_raw_w[:].rearrange("p (a c) -> p a c", a=PASSES),
-            in_=wb_words.rearrange("a p c i -> p a (c i)").bitcast(I32),
-        )
-        load_scales(wb_scales, wb_raw_s)
+        def load_wb(a):
+            nc.sync.dma_start(
+                out=wb_raw_w[:, a * K : (a + 1) * K], in_=wb_words[a].rearrange("p c i -> p (c i)").bitcast(I32)
+            )
+
+        def load_table(a):
+            tab_w[a] = staged("tab_w", I32)
+            nc.sync.dma_start(out=tab_w[a][:], in_=tab_words[a].rearrange("p c i -> p (c i)").bitcast(I32))
+
+        def load_list():
+            nc.sync.dma_start(idx[:], offs)
+
+        def load_placing():
+            nc.sync.dma_start(idx2[:], offs2)
+            nc.sync.dma_start(
+                out=gain_t[:].rearrange("p (b t) -> p b t", t=PACK),
+                in_=gain.rearrange("(b p t) -> p b t", p=P, t=PACK),
+            )
+            for q in range(4):
+                nc.sync.dma_start(out=wgo_t[32 * q : 32 * (q + 1), :], in_=wgo.rearrange("(p t) j -> p (t j)", t=PACK))
 
         def gather_table(a):
             nc.vector.tensor_copy(v_w[a][:], tab_w[a][:].bitcast(U32).indirect(idx[:]))
+
+        def order_wb(a):
+            nc.vector.tensor_copy(
+                wb_w[a][:].rearrange("p (g t c i) -> p g c t i", t=PACK, i=4, c=P // 4),
+                wb_raw_w[:, a * K : (a + 1) * K].rearrange("p (g c i t) -> p g c t i", t=PACK, i=4, c=P // 4),
+            )
+
+        def gather_table_scales(a):
             nc.vector.tensor_copy(v_s[a][:], tab_s[:, a * T : (a + 1) * T].indirect(idx[:]))
 
-        def order_wb():
-            for src, dst in ((wb_raw_w, wb_w), (wb_raw_s, wb_s)):
-                nc.vector.tensor_copy(
-                    dst[:].rearrange("p (g t m) -> p g m t", t=PACK, m=P),
-                    src[:].rearrange("p (g m t) -> p g m t", t=PACK, m=P),
-                )
+        def order_wb_scales(a):
+            nc.vector.tensor_copy(
+                wb_s[a][:].rearrange("p (g t m) -> p g t m", t=PACK, m=P),
+                wb_raw_s[:, a * K : (a + 1) * K].rearrange("p (g m t) -> p g t m", t=PACK, m=P),
+            )
 
         wa_bf = {}
 
@@ -126,8 +145,8 @@ def tile_list_slope_weighted_commutator_kernel(
             if w == "a":
                 cols = slice(t * P, (t + 1) * P)
                 return wa_w[a, b][:, cols].bitcast(E4M3), wa_s[a, b][:, cols]
-            c0 = a * K + b * SPAN + t * P
-            return wb_w[:, c0 : c0 + P].bitcast(E4M3), wb_s[:, c0 : c0 + P]
+            c0 = b * SPAN + t * P
+            return wb_w[a][:, c0 : c0 + P].bitcast(E4M3), wb_s[a][:, c0 : c0 + P]
 
         first = {}
 
@@ -162,9 +181,9 @@ def tile_list_slope_weighted_commutator_kernel(
             slp = nd[b, t][:, j0:j1].rearrange("p (h j) -> p h j", j=HALF)
             nc.vector.scalar_tensor_tensor(dst, acc, -1.0 if w == "b" else 1.0, slp, MULT, MULT)
 
-        def weave(engine_copy, w, b, j0, j1):
+        def weave(w, b, j0, j1, copy):
             cols = slice(PACK * j0, PACK * j1)
-            engine_copy(
+            copy(
                 woven[w, b][:, cols].rearrange("p (h c i t) -> p h c t i", t=PACK, i=4, c=HALF // 4),
                 planes[w, b][:, cols].rearrange("p (h t c i) -> p h c t i", t=PACK, i=4, c=HALF // 4),
             )
@@ -209,89 +228,90 @@ def tile_list_slope_weighted_commutator_kernel(
                 out=out.rearrange("(b p t) c -> b t p c", p=P, t=PACK)[b, t], in_=windows[n % WINDOWS][:]
             )
 
-        def slice_step(b, t):
-            gather_rows(b, t, 0, S)
-            slope(b, t, 0, S)
-
-        load_wa(0, 0)
-        load_rows(0, 0)
-        load_wa(1, 0)
-        load_rows(0, 1)
-        load_rows(0, 2)
-        load_rows(0, 3)
-        load_wa(0, 1)
+        load_list()
+        load_scales(tab_scales, tab_s)
+        wb_raw_w = staged("wb_raw_w", I32)
+        load_wb(0)
+        load_wb(1)
+        load_table(0)
+        load_scales(wb_scales, wb_raw_s)
+        load_table(1)
+        for t, (a, b) in enumerate(blocks):
+            load_rows(0, t)
+            load_wa(a, b)
         load_rows(1, 0)
-        load_wa(1, 1)
-        load_rows(1, 1)
 
+        for a in range(PASSES):
+            gather_table_scales(a)
+        for a in range(PASSES):
+            order_wb(a)
+        load_rows(1, 1)
         gather_table(0)
+        load_rows(1, 2)
+        for a in range(PASSES):
+            order_wb_scales(a)
         gather_table(1)
-        order_wb()
-        cast_wa(0, 0)
-        cast_wa(1, 0)
+        load_rows(1, 3)
         for t in range(PACK):
             stage1("b", 0, t)
-        slice_step(0, 0)
-        load_rows(1, 2)
+
+        gather_rows(0, 0, 0, S)
+        slope(0, 0, 0, S)
+        wgo_t = staged("wgo_t", F32)
+        load_placing()
+        cast_wa(0, 0)
+        gather_rows(0, 1, 0, S)
         quantise_wa(0, 0)
         weigh("b", 0, 0, 0, S)
-        slice_step(0, 1)
-        load_rows(1, 3)
-        nc.sync.dma_start(idx2[:], offs2)
-        nc.sync.dma_start(
-            out=gain_t[:].rearrange("p (b t) -> p b t", t=PACK),
-            in_=gain.rearrange("(b p t) -> p b t", p=P, t=PACK),
-        )
-        for q in range(4):
-            nc.sync.dma_start(out=wgo_t[32 * q : 32 * (q + 1), :], in_=wgo.rearrange("(p t) j -> p (t j)", t=PACK))
+        slope(0, 1, 0, S)
+        cast_wa(1, 0)
+        gather_rows(0, 2, 0, S)
         quantise_wa(1, 0)
-        weigh("b", 0, 1, 0, S)
         for t in range(PACK):
             stage1("a", 0, t)
-        slice_step(0, 2)
+        weigh("b", 0, 1, 0, S)
+        slope(0, 2, 0, S)
         weigh("a", 0, 0, 0, S)
-        weigh("b", 0, 2, 0, S)
         weigh("a", 0, 1, 0, S)
-        weigh("a", 0, 2, 0, S)
-        slice_step(0, 3)
         cast_wa(0, 1)
-        weigh("b", 0, 3, 0, S)
-        weigh("a", 0, 3, 0, S)
-        weave(nc.scalar.copy, "b", 0, 0, S)
+        gather_rows(0, 3, 0, S)
+        quantise_wa(0, 1)
+        weigh("b", 0, 2, 0, S)
+        weigh("a", 0, 2, 0, S)
+        slope(0, 3, 0, S)
+        cast_wa(1, 1)
+        gather_rows(1, 0, 0, S)
+        quantise_wa(1, 1)
+        for w in "ba":
+            weigh(w, 0, 3, 0, S)
+            weave(w, 0, 0, S, nc.scalar.copy)
         for t in range(PACK):
             stage1("b", 1, t)
-        slice_step(1, 0)
-        cast_wa(1, 1)
-        quantise_wa(0, 1)
-        weigh("b", 1, 0, 0, S)
-        quantise_h("b", 0, 0, S)
-        weave(nc.scalar.copy, "a", 0, 0, S)
-        slice_step(1, 1)
-        quantise_wa(1, 1)
-        weigh("b", 1, 1, 0, S)
-        for t in range(PACK):
             stage1("a", 1, t)
-        slice_step(1, 2)
-        weigh("a", 1, 0, 0, S)
-        weigh("b", 1, 2, 0, S)
-        weigh("a", 1, 1, 0, S)
-        weigh("a", 1, 2, 0, S)
-        quantise_h("a", 0, 0, S)
+        slope(1, 0, 0, S)
+        for t, w in ((1, "b"), (2, "a")):
+            gather_rows(1, t, 0, S)
+            weigh("b", 1, t - 1, 0, S)
+            weigh("a", 1, t - 1, 0, S)
+            slope(1, t, 0, S)
+            quantise_h(w, 0, 0, S)
 
-        halves = [(0, HALF), (HALF, S)]
-        for j0, j1 in halves:
-            gather_rows(1, 3, j0, j1)
-        for j0, j1 in halves:
-            slope(1, 3, j0, j1)
-        for j0, j1 in halves:
-            weigh("b", 1, 3, j0, j1)
-            weigh("a", 1, 3, j0, j1)
-        weave(nc.scalar.copy, "b", 1, 0, HALF)
-        weave(nc.scalar.copy, "b", 1, HALF, S)
-        weave(nc.vector.tensor_copy, "a", 1, 0, HALF)
+        gather_rows(1, 3, 0, HALF)
+        weigh("b", 1, 2, 0, S)
+        weigh("a", 1, 2, 0, S)
+        slope(1, 3, 0, HALF)
+        gather_rows(1, 3, HALF, S)
+        weigh("b", 1, 3, 0, HALF)
+        weave("b", 1, 0, HALF, nc.scalar.copy)
+        weigh("a", 1, 3, 0, HALF)
+        slope(1, 3, HALF, S)
+        weave("a", 1, 0, HALF, nc.vector.tensor_copy)
+        weigh("b", 1, 3, HALF, S)
+        weigh("a", 1, 3, HALF, S)
+        weave("b", 1, HALF, S, nc.scalar.copy)
         quantise_h("b", 1, 0, HALF)
         quantise_h("a", 1, 0, HALF)
-        weave(nc.vector.tensor_copy, "a", 1, HALF, S)
+        weave("a", 1, HALF, S, nc.vector.tensor_copy)
         order = [(b, t) for t in range(PACK) for b in range(PASSES)]
         stage2(0, *order[0], 0, HALF)
         stage2(1, *order[1], 0, HALF)

@@ -67,10 +67,10 @@ def tile_list_slope_weighted_commutator_kernel(
             nc.vector.memset(window[:], 0.0)
 
         def load_scales(src, dst):
-            for q in range(4):
+            for r in range(4):
                 nc.sync.dma_start(
-                    out=dst[32 * q : 32 * q + 4, :].bitcast(I32).rearrange("p (a c) -> p a c", a=PASSES),
-                    in_=src[:, 4 * q : 4 * q + 4, :].rearrange("a r c -> r a c").bitcast(I32),
+                    out=dst[r:P:32, :].bitcast(I32).rearrange("p (a c) -> p a c", a=PASSES),
+                    in_=src.rearrange("a (q r) c -> r q a c", r=4)[r].bitcast(I32),
                 )
 
         def staged(name, dtype):
@@ -200,7 +200,8 @@ def tile_list_slope_weighted_commutator_kernel(
 
         def stage2(unit, b, t, j0, j1):
             acc = psum.tile([P, j1 - j0], F32, name="second", tag=banks[unit % len(banks)])
-            for n, (w, r) in enumerate(prods):
+            passes = prods if j1 - j0 == HALF else prods[::-1]
+            for n, (w, r) in enumerate(passes):
                 codes, scales = weights("a" if w == "b" else "b", r, b, t)
                 nc.tensor.matmul_mx(
                     out=acc[:],
@@ -229,9 +230,9 @@ def tile_list_slope_weighted_commutator_kernel(
             )
 
         load_list()
-        load_scales(tab_scales, tab_s)
         wb_raw_w = staged("wb_raw_w", I32)
         load_wb(0)
+        load_scales(tab_scales, tab_s)
         load_wb(1)
         load_table(0)
         load_scales(wb_scales, wb_raw_s)
@@ -241,10 +242,10 @@ def tile_list_slope_weighted_commutator_kernel(
             load_wa(a, b)
         load_rows(1, 0)
 
+        order_wb(0)
         for a in range(PASSES):
             gather_table_scales(a)
-        for a in range(PASSES):
-            order_wb(a)
+        order_wb(1)
         load_rows(1, 1)
         gather_table(0)
         load_rows(1, 2)

@@ -237,16 +237,17 @@ def tile_list_slope_weighted_commutator_kernel(
         load_table(0)
         load_scales(wb_scales, wb_raw_s)
         load_table(1)
-        for t, (a, b) in enumerate(blocks):
-            load_rows(0, t)
-            load_wa(a, b)
-        load_rows(1, 0)
+        for b, t in slices[:3]:
+            load_rows(b, t)
+        for n in range(3):
+            load_wa(*blocks[n])
+            load_rows(*slices[3 + n])
 
         order_wb(0)
         for a in range(PASSES):
             gather_table_scales(a)
         order_wb(1)
-        load_rows(1, 1)
+        load_wa(1, 1)
         gather_table(0)
         load_rows(1, 2)
         for a in range(PASSES):
@@ -260,42 +261,44 @@ def tile_list_slope_weighted_commutator_kernel(
         slope(0, 0, 0, S)
         wgo_t = staged("wgo_t", F32)
         load_placing()
+        for t in (1, 2):
+            gather_rows(0, t, 0, S)
+            weigh("b", 0, t - 1, 0, S)
+            slope(0, t, 0, S)
         cast_wa(0, 0)
-        gather_rows(0, 1, 0, S)
-        quantise_wa(0, 0)
-        weigh("b", 0, 0, 0, S)
-        slope(0, 1, 0, S)
-        cast_wa(1, 0)
-        gather_rows(0, 2, 0, S)
-        quantise_wa(1, 0)
-        for t in range(PACK):
-            stage1("a", 0, t)
-        weigh("b", 0, 1, 0, S)
-        slope(0, 2, 0, S)
-        weigh("a", 0, 0, 0, S)
-        weigh("a", 0, 1, 0, S)
-        cast_wa(0, 1)
         gather_rows(0, 3, 0, S)
-        quantise_wa(0, 1)
+        quantise_wa(0, 0)
         weigh("b", 0, 2, 0, S)
-        weigh("a", 0, 2, 0, S)
         slope(0, 3, 0, S)
-        cast_wa(1, 1)
+        cast_wa(1, 0)
         gather_rows(1, 0, 0, S)
-        quantise_wa(1, 1)
-        for w in "ba":
-            weigh(w, 0, 3, 0, S)
-            weave(w, 0, 0, S, nc.scalar.copy)
+        quantise_wa(1, 0)
+        weigh("b", 0, 3, 0, S)
+        weave("b", 0, 0, S, nc.scalar.copy)
         for t in range(PACK):
             stage1("b", 1, t)
-            stage1("a", 1, t)
+        for t in range(PACK):
+            stage1("a", 0, t)
         slope(1, 0, 0, S)
-        for t, w in ((1, "b"), (2, "a")):
-            gather_rows(1, t, 0, S)
-            weigh("b", 1, t - 1, 0, S)
-            weigh("a", 1, t - 1, 0, S)
-            slope(1, t, 0, S)
-            quantise_h(w, 0, 0, S)
+        for t in range(PACK):
+            weigh("a", 0, t, 0, S)
+        cast_wa(0, 1)
+        weave("a", 0, 0, S, nc.scalar.copy)
+        gather_rows(1, 1, 0, S)
+        quantise_wa(0, 1)
+        quantise_h("b", 0, 0, S)
+        weigh("b", 1, 0, 0, S)
+        slope(1, 1, 0, S)
+        cast_wa(1, 1)
+        quantise_h("a", 0, 0, S)
+        gather_rows(1, 2, 0, S)
+        quantise_wa(1, 1)
+        for t in range(PACK):
+            stage1("a", 1, t)
+        weigh("b", 1, 1, 0, S)
+        slope(1, 2, 0, S)
+        weigh("a", 1, 0, 0, S)
+        weigh("a", 1, 1, 0, S)
 
         gather_rows(1, 3, 0, HALF)
         weigh("b", 1, 2, 0, S)

@@ -21,8 +21,15 @@ P = 128
 PACK = 4
 SPAN = P * PACK
 PASSES = K // SPAN
+QUADS = 4
+QUAD = P // QUADS
+ROWS = 4
+LIVE = (QUADS - 1) * QUAD + ROWS
+RUN = 4
 HALF = S // 2
+STAGED = 12
 WINDOWS = 3
+SPLIT = 2
 
 
 def tile_list_slope_weighted_commutator_kernel(
@@ -31,7 +38,7 @@ def tile_list_slope_weighted_commutator_kernel(
     nc = tc.nc
     with ExitStack() as ctx:
         keep = ctx.enter_context(tc.tile_pool(name="keep", bufs=1))
-        stage = ctx.enter_context(tc.tile_pool(name="stage", bufs=12))
+        stage = ctx.enter_context(tc.tile_pool(name="stage", bufs=STAGED))
         cast = ctx.enter_context(tc.tile_pool(name="cast", bufs=2))
         res = ctx.enter_context(tc.tile_pool(name="res", bufs=3))
         psum = ctx.enter_context(tc.psum_pool(name="psum", bufs=1))
@@ -39,42 +46,35 @@ def tile_list_slope_weighted_commutator_kernel(
         def kept(name, width, dtype):
             return keep.tile([P, width], dtype, name=name, align_bytes=64)
 
+        def staged(name, dtype):
+            return stage.tile([P, T], dtype, name=name, tag="staged", align_bytes=64)
+
         idx = keep.tile([P, S // 16], U16, name="idx")
         idx2 = keep.tile([P, S // 16], U16, name="idx2")
-        tab_s = kept("tab_s", PASSES * T, U8)
+        tab_s = kept("tab_s", T, U8)
         v_w = [kept("v_w%d" % a, S, U32) for a in range(PASSES)]
         v_s = [kept("v_s%d" % a, S, U8) for a in range(PASSES)]
         wb_raw_s = kept("wb_raw_s", PASSES * K, U8)
         wb_w = [kept("wb_w%d" % a, K, I32) for a in range(PASSES)]
         wb_s = [kept("wb_s%d" % a, K, U8) for a in range(PASSES)]
-        blocks = [(a, b) for b in range(PASSES) for a in range(PASSES)]
-        wa_w = {ab: kept("wa_w%d%d" % ab, SPAN, U32) for ab in blocks}
-        wa_s = {ab: kept("wa_s%d%d" % ab, SPAN, U8) for ab in blocks}
+        wa_parts = [(a, b) for b in range(PASSES) for a in range(PASSES)]
+        wa_w = {ab: kept("wa_w%d%d" % ab, SPAN, U32) for ab in wa_parts}
+        wa_s = {ab: kept("wa_s%d%d" % ab, SPAN, U8) for ab in wa_parts}
         slices = [(b, t) for b in range(PASSES) for t in range(PACK)]
         nd = {bt: kept("nd%d%d" % bt, S, F32) for bt in slices}
         prods = [(w, b) for b in range(PASSES) for w in "ba"]
-        planes = {wb_: kept("planes%s%d" % wb_, PACK * S, BF16) for wb_ in prods}
-        woven = {wb_: kept("woven%s%d" % wb_, PACK * S, BF16) for wb_ in prods}
-        h_w = {wb_: kept("h_w%s%d" % wb_, S, U32) for wb_ in prods}
-        h_s = {wb_: kept("h_s%s%d" % wb_, S, U8) for wb_ in prods}
+        apart = {key: kept("planes%s%d" % key, PACK * S, BF16) for key in prods}
+        woven = {key: kept("woven%s%d" % key, PACK * S, BF16) for key in prods}
+        h_w = {key: kept("h_w%s%d" % key, S, U32) for key in prods}
+        h_s = {key: kept("h_s%s%d" % key, S, U8) for key in prods}
         gain_t = kept("gain_t", PASSES * PACK, F32)
         windows = [kept("window%d" % i, T2, F32) for i in range(WINDOWS)]
 
-        nc.gpsimd.memset(tab_s[:, :T].bitcast(I32), 0)
-        nc.vector.memset(tab_s[:, T:].bitcast(I32), 0)
+        nc.gpsimd.memset(tab_s[:].bitcast(I32), 0)
+        nc.gpsimd.memset(v_s[1][:].bitcast(I32), 0)
         nc.vector.memset(wb_raw_s[:].bitcast(I32), 0)
         for window in windows:
             nc.vector.memset(window[:], 0.0)
-
-        def load_scales(src, dst):
-            for r in range(4):
-                nc.sync.dma_start(
-                    out=dst[r:P:32, :].bitcast(I32).rearrange("p (a c) -> p a c", a=PASSES),
-                    in_=src.rearrange("a (q r) c -> r q a c", r=4)[r].bitcast(I32),
-                )
-
-        def staged(name, dtype):
-            return stage.tile([P, T], dtype, name=name, tag="staged", align_bytes=64)
 
         s_rows, wa_raw, tab_w = {}, {}, {}
 
@@ -94,12 +94,23 @@ def tile_list_slope_weighted_commutator_kernel(
                 out=wb_raw_w[:, a * K : (a + 1) * K], in_=wb_words[a].rearrange("p c i -> p (c i)").bitcast(I32)
             )
 
+        def load_wb_scales():
+            for r in range(ROWS):
+                nc.sync.dma_start(
+                    out=wb_raw_s[r:P:QUAD, :].bitcast(I32).rearrange("p (a c) -> p a c", a=PASSES),
+                    in_=wb_scales.rearrange("a (q r) c -> r q a c", r=ROWS)[r].bitcast(I32),
+                )
+
         def load_table(a):
             tab_w[a] = staged("tab_w", I32)
             nc.sync.dma_start(out=tab_w[a][:], in_=tab_words[a].rearrange("p c i -> p (c i)").bitcast(I32))
 
-        def load_list():
-            nc.sync.dma_start(idx[:], offs)
+        def load_table_scales():
+            for q in range(QUADS):
+                nc.sync.dma_start(
+                    out=tab_s[QUAD * q : QUAD * q + ROWS * PASSES, :].bitcast(I32),
+                    in_=tab_scales[:, ROWS * q : ROWS * (q + 1), :].bitcast(I32),
+                )
 
         def load_placing():
             nc.sync.dma_start(idx2[:], offs2)
@@ -107,20 +118,23 @@ def tile_list_slope_weighted_commutator_kernel(
                 out=gain_t[:].rearrange("p (b t) -> p b t", t=PACK),
                 in_=gain.rearrange("(b p t) -> p b t", p=P, t=PACK),
             )
-            for q in range(4):
-                nc.sync.dma_start(out=wgo_t[32 * q : 32 * (q + 1), :], in_=wgo.rearrange("(p t) j -> p (t j)", t=PACK))
+            for q in range(QUADS):
+                nc.sync.dma_start(
+                    out=wgo_t[QUAD * q : QUAD * (q + 1), :], in_=wgo.rearrange("(p t) j -> p (t j)", t=PACK)
+                )
 
         def gather_table(a):
             nc.vector.tensor_copy(v_w[a][:], tab_w[a][:].bitcast(U32).indirect(idx[:]))
 
+        def gather_table_scales():
+            nc.vector.tensor_copy(v_s[0][:], tab_s[:].indirect(idx[:]))
+            nc.sync.dma_start(out=v_s[1][0:LIVE, :].bitcast(I32), in_=v_s[0][ROWS : ROWS + LIVE, :].bitcast(I32))
+
         def order_wb(a):
             nc.vector.tensor_copy(
-                wb_w[a][:].rearrange("p (g t c i) -> p g c t i", t=PACK, i=4, c=P // 4),
-                wb_raw_w[:, a * K : (a + 1) * K].rearrange("p (g c i t) -> p g c t i", t=PACK, i=4, c=P // 4),
+                wb_w[a][:].rearrange("p (g t c i) -> p g c t i", t=PACK, i=RUN, c=P // RUN),
+                wb_raw_w[:, a * K : (a + 1) * K].rearrange("p (g c i t) -> p g c t i", t=PACK, i=RUN, c=P // RUN),
             )
-
-        def gather_table_scales(a):
-            nc.vector.tensor_copy(v_s[a][:], tab_s[:, a * T : (a + 1) * T].indirect(idx[:]))
 
         def order_wb_scales(a):
             nc.vector.tensor_copy(
@@ -150,19 +164,20 @@ def tile_list_slope_weighted_commutator_kernel(
 
         first = {}
 
-        def stage1(w, b, t):
-            first[w, b, t] = psum.tile([P, S], F32, name="first", tag="bank%s%d" % (w, t))
-            for a in range(PASSES):
-                codes, scales = weights(w, a, b, t)
-                nc.tensor.matmul_mx(
-                    out=first[w, b, t][:],
-                    lhsT=codes,
-                    lhsT_scale=scales,
-                    rhs=v_w[a][:].bitcast(E5M2),
-                    rhs_scale=v_s[a][:],
-                    start=(a == 0),
-                    stop=(a == PASSES - 1),
-                )
+        def stage1(w, b):
+            for t in range(PACK):
+                first[w, b, t] = psum.tile([P, S], F32, name="first", tag="bank%s%d" % (w, t))
+                for a in range(PASSES):
+                    codes, scales = weights(w, a, b, t)
+                    nc.tensor.matmul_mx(
+                        out=first[w, b, t][:],
+                        lhsT=codes,
+                        lhsT_scale=scales,
+                        rhs=v_w[a][:].bitcast(E5M2),
+                        rhs_scale=v_s[a][:],
+                        start=(a == 0),
+                        stop=(a == PASSES - 1),
+                    )
 
         picked = {}
 
@@ -176,16 +191,22 @@ def tile_list_slope_weighted_commutator_kernel(
 
         def weigh(w, b, t, j0, j1):
             h0, h1 = j0 // HALF, j1 // HALF
-            dst = planes[w, b][:].rearrange("p (h t j) -> p h t j", t=PACK, j=HALF)[:, h0:h1, t, :]
+            dst = apart[w, b][:].rearrange("p (h t j) -> p h t j", t=PACK, j=HALF)[:, h0:h1, t, :]
             acc = first[w, b, t][:, j0:j1].rearrange("p (h j) -> p h j", j=HALF)
             slp = nd[b, t][:, j0:j1].rearrange("p (h j) -> p h j", j=HALF)
             nc.vector.scalar_tensor_tensor(dst, acc, -1.0 if w == "b" else 1.0, slp, MULT, MULT)
 
+        def slope_step(b, t, *between):
+            gather_rows(b, t, 0, S)
+            for key in between:
+                weigh(*key, 0, S)
+            slope(b, t, 0, S)
+
         def weave(w, b, j0, j1, copy):
             cols = slice(PACK * j0, PACK * j1)
             copy(
-                woven[w, b][:, cols].rearrange("p (h c i t) -> p h c t i", t=PACK, i=4, c=HALF // 4),
-                planes[w, b][:, cols].rearrange("p (h t c i) -> p h c t i", t=PACK, i=4, c=HALF // 4),
+                woven[w, b][:, cols].rearrange("p (h c i t) -> p h c t i", t=PACK, i=RUN, c=HALF // RUN),
+                apart[w, b][:, cols].rearrange("p (h t c i) -> p h c t i", t=PACK, i=RUN, c=HALF // RUN),
             )
 
         def quantise_h(w, b, j0, j1):
@@ -198,8 +219,8 @@ def tile_list_slope_weighted_commutator_kernel(
         banks = ["bank%s%d" % (w, t) for t in range(PACK) for w in "ba"]
         y = {}
 
-        def stage2(unit, b, t, j0, j1):
-            acc = psum.tile([P, j1 - j0], F32, name="second", tag=banks[unit % len(banks)])
+        def stage2(turn, b, t, j0, j1):
+            acc = psum.tile([P, j1 - j0], F32, name="second", tag=banks[turn % len(banks)])
             passes = prods if j1 - j0 == HALF else prods[::-1]
             for n, (w, r) in enumerate(passes):
                 codes, scales = weights("a" if w == "b" else "b", r, b, t)
@@ -229,23 +250,27 @@ def tile_list_slope_weighted_commutator_kernel(
                 out=out.rearrange("(b p t) c -> b t p c", p=P, t=PACK)[b, t], in_=windows[n % WINDOWS][:]
             )
 
-        load_list()
+        nc.sync.dma_start(idx[:], offs)
         wb_raw_w = staged("wb_raw_w", I32)
         load_wb(0)
-        load_scales(tab_scales, tab_s)
+        load_table_scales()
         load_wb(1)
         load_table(0)
-        load_scales(wb_scales, wb_raw_s)
+        load_wb_scales()
         load_table(1)
-        for b, t in slices[:3]:
-            load_rows(b, t)
-        for n in range(3):
-            load_wa(*blocks[n])
-            load_rows(*slices[3 + n])
-
         order_wb(0)
-        for a in range(PASSES):
-            gather_table_scales(a)
+        gather_table_scales()
+
+        load_rows(0, 0)
+        load_rows(0, 1)
+        load_wa(0, 0)
+        load_rows(0, 2)
+        load_wa(1, 0)
+        load_rows(0, 3)
+        load_rows(1, 0)
+        load_wa(0, 1)
+        load_rows(1, 1)
+
         order_wb(1)
         load_wa(1, 1)
         gather_table(0)
@@ -254,80 +279,66 @@ def tile_list_slope_weighted_commutator_kernel(
             order_wb_scales(a)
         gather_table(1)
         load_rows(1, 3)
-        for t in range(PACK):
-            stage1("b", 0, t)
+        stage1("b", 0)
 
-        gather_rows(0, 0, 0, S)
-        slope(0, 0, 0, S)
+        slope_step(0, 0)
         wgo_t = staged("wgo_t", F32)
         load_placing()
-        for t in (1, 2):
-            gather_rows(0, t, 0, S)
-            weigh("b", 0, t - 1, 0, S)
-            slope(0, t, 0, S)
+        slope_step(0, 1, ("b", 0, 0))
         cast_wa(0, 0)
-        gather_rows(0, 3, 0, S)
+        slope_step(0, 2, ("b", 0, 1))
         quantise_wa(0, 0)
-        weigh("b", 0, 2, 0, S)
-        slope(0, 3, 0, S)
         cast_wa(1, 0)
-        gather_rows(1, 0, 0, S)
+        slope_step(0, 3, ("b", 0, 2))
         quantise_wa(1, 0)
+        stage1("a", 0)
         weigh("b", 0, 3, 0, S)
         weave("b", 0, 0, S, nc.scalar.copy)
-        for t in range(PACK):
-            stage1("b", 1, t)
-        for t in range(PACK):
-            stage1("a", 0, t)
-        slope(1, 0, 0, S)
-        for t in range(PACK):
+
+        stage1("b", 1)
+        slope_step(1, 0, ("a", 0, 0))
+        for t in range(1, PACK):
             weigh("a", 0, t, 0, S)
         cast_wa(0, 1)
         weave("a", 0, 0, S, nc.scalar.copy)
-        gather_rows(1, 1, 0, S)
-        quantise_wa(0, 1)
+        slope_step(1, 1, ("b", 1, 0))
         quantise_h("b", 0, 0, S)
-        weigh("b", 1, 0, 0, S)
-        slope(1, 1, 0, S)
+        quantise_wa(0, 1)
         cast_wa(1, 1)
-        quantise_h("a", 0, 0, S)
-        gather_rows(1, 2, 0, S)
+        slope_step(1, 2, ("b", 1, 1))
         quantise_wa(1, 1)
-        for t in range(PACK):
-            stage1("a", 1, t)
-        weigh("b", 1, 1, 0, S)
-        slope(1, 2, 0, S)
-        weigh("a", 1, 0, 0, S)
-        weigh("a", 1, 1, 0, S)
+        stage1("a", 1)
+        quantise_h("a", 0, 0, S)
 
-        gather_rows(1, 3, 0, HALF)
-        weigh("b", 1, 2, 0, S)
-        weigh("a", 1, 2, 0, S)
-        slope(1, 3, 0, HALF)
-        gather_rows(1, 3, HALF, S)
-        weigh("b", 1, 3, 0, HALF)
+        last = PACK - 1
+        gather_rows(1, last, 0, HALF)
+        weigh("b", 1, last - 1, 0, S)
+        slope(1, last, 0, HALF)
+        gather_rows(1, last, HALF, S)
+        weigh("b", 1, last, 0, HALF)
         weave("b", 1, 0, HALF, nc.scalar.copy)
-        weigh("a", 1, 3, 0, HALF)
-        slope(1, 3, HALF, S)
+        slope(1, last, HALF, S)
+        for t in range(last):
+            weigh("a", 1, t, 0, S)
+        weigh("a", 1, last, 0, HALF)
+        weigh("b", 1, last, HALF, S)
         weave("a", 1, 0, HALF, nc.vector.tensor_copy)
-        weigh("b", 1, 3, HALF, S)
-        weigh("a", 1, 3, HALF, S)
         weave("b", 1, HALF, S, nc.scalar.copy)
         quantise_h("b", 1, 0, HALF)
         quantise_h("a", 1, 0, HALF)
+        weigh("a", 1, last, HALF, S)
         weave("a", 1, HALF, S, nc.vector.tensor_copy)
-        order = [(b, t) for t in range(PACK) for b in range(PASSES)]
-        stage2(0, *order[0], 0, HALF)
-        stage2(1, *order[1], 0, HALF)
-        place(0, *order[0], 0, HALF)
+
+        outputs = [(b, t) for t in range(PACK) for b in range(PASSES)]
+        for n in range(SPLIT):
+            stage2(n, *outputs[n], 0, HALF)
+        place(0, *outputs[0], 0, HALF)
         quantise_h("b", 1, HALF, S)
         quantise_h("a", 1, HALF, S)
-        place(1, *order[1], 0, HALF)
-        for n in range(2):
-            stage2(2 + n, *order[n], HALF, S)
-            place(n, *order[n], HALF, S)
-            store(n, *order[n])
-        for n in range(2, len(order)):
-            stage2(2 + n, *order[n], 0, S)
-            place(n, *order[n], 0, S)
-            store(n, *order[n])
+        for n in range(1, SPLIT):
+            place(n, *outputs[n], 0, HALF)
+        for n in range(len(outputs)):
+            j0 = HALF if n < SPLIT else 0
+            stage2(SPLIT + n, *outputs[n], j0, S)
+            place(n, *outputs[n], j0, S)
+            store(n, *outputs[n])

@@ -27,7 +27,6 @@ ROWS = 4
 LIVE = (QUADS - 1) * QUAD + ROWS
 RUN = 4
 HALF = S // 2
-STAGED = 12
 WINDOWS = 3
 SPLIT = 2
 
@@ -38,108 +37,99 @@ def tile_list_slope_weighted_commutator_kernel(
     nc = tc.nc
     with ExitStack() as ctx:
         keep = ctx.enter_context(tc.tile_pool(name="keep", bufs=1))
-        stage = ctx.enter_context(tc.tile_pool(name="stage", bufs=STAGED))
         cast = ctx.enter_context(tc.tile_pool(name="cast", bufs=2))
-        res = ctx.enter_context(tc.tile_pool(name="res", bufs=3))
+        res = ctx.enter_context(tc.tile_pool(name="res", bufs=4))
         psum = ctx.enter_context(tc.psum_pool(name="psum", bufs=1))
 
-        def kept(name, width, dtype):
-            return keep.tile([P, width], dtype, name=name, align_bytes=64)
-
-        def staged(name, dtype):
-            return stage.tile([P, T], dtype, name=name, tag="staged", align_bytes=64)
+        def kept(name, width, dtype, tag=None):
+            return keep.tile([P, width], dtype, name=name, tag=tag or name, align_bytes=64)
 
         idx = keep.tile([P, S // 16], U16, name="idx")
         idx2 = keep.tile([P, S // 16], U16, name="idx2")
-        tab_s = kept("tab_s", T, U8)
+        tab_s = kept("tab_s", PASSES * T, U8)
         v_w = [kept("v_w%d" % a, S, U32) for a in range(PASSES)]
         v_s = [kept("v_s%d" % a, S, U8) for a in range(PASSES)]
         wb_raw_s = kept("wb_raw_s", PASSES * K, U8)
-        wb_w = [kept("wb_w%d" % a, K, I32) for a in range(PASSES)]
-        wb_s = [kept("wb_s%d" % a, K, U8) for a in range(PASSES)]
+        wb_w = [kept("wb_w%d" % b, PASSES * SPAN, I32) for b in range(PASSES)]
+        wb_s = kept("wb_s", PASSES * K, U8)
         wa_parts = [(a, b) for b in range(PASSES) for a in range(PASSES)]
         wa_w = {ab: kept("wa_w%d%d" % ab, SPAN, U32) for ab in wa_parts}
         wa_s = {ab: kept("wa_s%d%d" % ab, SPAN, U8) for ab in wa_parts}
         slices = [(b, t) for b in range(PASSES) for t in range(PACK)]
         nd = {bt: kept("nd%d%d" % bt, S, F32) for bt in slices}
         prods = [(w, b) for b in range(PASSES) for w in "ba"]
-        apart = {key: kept("planes%s%d" % key, PACK * S, BF16) for key in prods}
-        woven = {key: kept("woven%s%d" % key, PACK * S, BF16) for key in prods}
         h_w = {key: kept("h_w%s%d" % key, S, U32) for key in prods}
         h_s = {key: kept("h_s%s%d" % key, S, U8) for key in prods}
         gain_t = kept("gain_t", PASSES * PACK, F32)
+        wgo_t = [kept("wgo_first", S, F32), kept("wgo_rest", (PACK - 1) * S, F32)]
         windows = [kept("window%d" % i, T2, F32) for i in range(WINDOWS)]
 
         nc.gpsimd.memset(tab_s[:].bitcast(I32), 0)
-        nc.gpsimd.memset(v_s[1][:].bitcast(I32), 0)
         nc.vector.memset(wb_raw_s[:].bitcast(I32), 0)
         for window in windows:
             nc.vector.memset(window[:], 0.0)
 
-        s_rows, wa_raw, tab_w = {}, {}, {}
+        s_rows, wa_raw, tab_w, wb_raw_w = {}, {}, {}, {}
 
         def load_rows(b, t):
-            s_rows[b, t] = staged("s_rows", F32)
+            s_rows[b, t] = kept("s_rows%d%d" % (b, t), T, F32)
             nc.sync.dma_start(out=s_rows[b, t][:], in_=sT.rearrange("(b p t) c -> b t p c", p=P, t=PACK)[b, t])
 
-        def load_wa(a, b):
-            wa_raw[a, b] = staged("wa_raw", F32)
+        def load_wa(a, b, i0=0, i1=PACK):
+            if i0 == 0:
+                wa_raw[a, b] = kept("wa_raw%d%d" % (a, b), PACK * SPAN, F32)
+            rows = wa[a * SPAN : (a + 1) * SPAN, b * SPAN : (b + 1) * SPAN].rearrange("(p i) c -> p i c", i=PACK)
             nc.sync.dma_start(
-                out=wa_raw[a, b][:].rearrange("p (i c) -> p i c", i=PACK),
-                in_=wa[a * SPAN : (a + 1) * SPAN, b * SPAN : (b + 1) * SPAN].rearrange("(p i) c -> p i c", i=PACK),
+                out=wa_raw[a, b][:, i0 * SPAN : i1 * SPAN].rearrange("p (i c) -> p i c", c=SPAN), in_=rows[:, i0:i1, :]
             )
 
-        def load_wb(a):
+        def load_wb(b):
+            wb_raw_w[b] = kept("wb_raw_w%d" % b, PASSES * SPAN, I32)
             nc.sync.dma_start(
-                out=wb_raw_w[:, a * K : (a + 1) * K], in_=wb_words[a].rearrange("p c i -> p (c i)").bitcast(I32)
+                out=wb_raw_w[b][:].rearrange("p (a c) -> p a c", a=PASSES),
+                in_=wb_words[:, :, b * SPAN : (b + 1) * SPAN, :].rearrange("a p c i -> p a (c i)").bitcast(I32),
             )
 
-        def load_wb_scales():
+        def load_scales(plane, scales):
             for r in range(ROWS):
                 nc.sync.dma_start(
-                    out=wb_raw_s[r:P:QUAD, :].bitcast(I32).rearrange("p (a c) -> p a c", a=PASSES),
-                    in_=wb_scales.rearrange("a (q r) c -> r q a c", r=ROWS)[r].bitcast(I32),
+                    out=plane[r:P:QUAD, :].bitcast(I32).rearrange("p (a c) -> p a c", a=PASSES),
+                    in_=scales.rearrange("a (q r) c -> r q a c", r=ROWS)[r].bitcast(I32),
                 )
 
         def load_table(a):
-            tab_w[a] = staged("tab_w", I32)
+            tab_w[a] = kept("tab_w%d" % a, T, I32)
             nc.sync.dma_start(out=tab_w[a][:], in_=tab_words[a].rearrange("p c i -> p (c i)").bitcast(I32))
 
-        def load_table_scales():
-            for q in range(QUADS):
-                nc.sync.dma_start(
-                    out=tab_s[QUAD * q : QUAD * q + ROWS * PASSES, :].bitcast(I32),
-                    in_=tab_scales[:, ROWS * q : ROWS * (q + 1), :].bitcast(I32),
-                )
-
-        def load_placing():
+        def load_small():
             nc.sync.dma_start(idx2[:], offs2)
             nc.sync.dma_start(
                 out=gain_t[:].rearrange("p (b t) -> p b t", t=PACK),
                 in_=gain.rearrange("(b p t) -> p b t", p=P, t=PACK),
             )
-            for q in range(QUADS):
-                nc.sync.dma_start(
-                    out=wgo_t[QUAD * q : QUAD * (q + 1), :], in_=wgo.rearrange("(p t) j -> p (t j)", t=PACK)
-                )
+
+        def load_placing():
+            rows = wgo.rearrange("(p t) j -> p (t j)", t=PACK)
+            for part, cols in enumerate((slice(0, S), slice(S, PACK * S))):
+                for q in range(QUADS):
+                    nc.sync.dma_start(out=wgo_t[part][QUAD * q : QUAD * (q + 1), :], in_=rows[:, cols])
 
         def gather_table(a):
             nc.vector.tensor_copy(v_w[a][:], tab_w[a][:].bitcast(U32).indirect(idx[:]))
 
-        def gather_table_scales():
-            nc.vector.tensor_copy(v_s[0][:], tab_s[:].indirect(idx[:]))
-            nc.sync.dma_start(out=v_s[1][0:LIVE, :].bitcast(I32), in_=v_s[0][ROWS : ROWS + LIVE, :].bitcast(I32))
+        def gather_table_scales(a):
+            nc.vector.tensor_copy(v_s[a][:], tab_s[:, a * T : (a + 1) * T].indirect(idx[:]))
 
-        def order_wb(a):
+        def order_wb(b):
             nc.vector.tensor_copy(
-                wb_w[a][:].rearrange("p (g t c i) -> p g c t i", t=PACK, i=RUN, c=P // RUN),
-                wb_raw_w[:, a * K : (a + 1) * K].rearrange("p (g c i t) -> p g c t i", t=PACK, i=RUN, c=P // RUN),
+                wb_w[b][:].rearrange("p (a t c i) -> p a c t i", t=PACK, i=RUN, c=P // RUN),
+                wb_raw_w[b][:].rearrange("p (a c i t) -> p a c t i", t=PACK, i=RUN, c=P // RUN),
             )
 
-        def order_wb_scales(a):
+        def order_wb_scales():
             nc.vector.tensor_copy(
-                wb_s[a][:].rearrange("p (g t m) -> p g t m", t=PACK, m=P),
-                wb_raw_s[:, a * K : (a + 1) * K].rearrange("p (g m t) -> p g t m", t=PACK, m=P),
+                wb_s[:].rearrange("p (g t m) -> p g t m", t=PACK, m=P),
+                wb_raw_s[:].rearrange("p (g m t) -> p g t m", t=PACK, m=P),
             )
 
         wa_bf = {}
@@ -159,27 +149,30 @@ def tile_list_slope_weighted_commutator_kernel(
             if w == "a":
                 cols = slice(t * P, (t + 1) * P)
                 return wa_w[a, b][:, cols].bitcast(E4M3), wa_s[a, b][:, cols]
-            c0 = b * SPAN + t * P
-            return wb_w[a][:, c0 : c0 + P].bitcast(E4M3), wb_s[a][:, c0 : c0 + P]
+            c0 = a * SPAN + t * P
+            s0 = a * K + b * SPAN + t * P
+            return wb_w[b][:, c0 : c0 + P].bitcast(E4M3), wb_s[:, s0 : s0 + P]
 
         first = {}
 
-        def stage1(w, b):
-            for t in range(PACK):
-                first[w, b, t] = psum.tile([P, S], F32, name="first", tag="bank%s%d" % (w, t))
-                for a in range(PASSES):
-                    codes, scales = weights(w, a, b, t)
-                    nc.tensor.matmul_mx(
-                        out=first[w, b, t][:],
-                        lhsT=codes,
-                        lhsT_scale=scales,
-                        rhs=v_w[a][:].bitcast(E5M2),
-                        rhs_scale=v_s[a][:],
-                        start=(a == 0),
-                        stop=(a == PASSES - 1),
-                    )
+        def stage1(ops, b):
+            for a in range(PASSES):
+                for t in range(PACK):
+                    for w in ops:
+                        if a == 0:
+                            first[w, b, t] = psum.tile([P, S], F32, name="first", tag="bank%s%d" % (w, t))
+                        codes, scales = weights(w, a, b, t)
+                        nc.tensor.matmul_mx(
+                            out=first[w, b, t][:],
+                            lhsT=codes,
+                            lhsT_scale=scales,
+                            rhs=v_w[a][:].bitcast(E5M2),
+                            rhs_scale=v_s[a][:],
+                            start=(a == 0),
+                            stop=(a == PASSES - 1),
+                        )
 
-        picked = {}
+        picked, apart, woven = {}, {}, {}
 
         def gather_rows(b, t, j0, j1):
             picked[b, t, j0] = res.tile([P, j1 - j0], F32, name="picked", tag="picked")
@@ -190,19 +183,27 @@ def tile_list_slope_weighted_commutator_kernel(
             nc.vector.scalar_tensor_tensor(nd[b, t][:, j0:j1], x, 1.0, x, SUB, MULT)
 
         def weigh(w, b, t, j0, j1):
+            if (w, b) not in apart:
+                apart[w, b] = kept("apart%s%d" % (w, b), PACK * S, BF16, tag="apart" + w)
             h0, h1 = j0 // HALF, j1 // HALF
             dst = apart[w, b][:].rearrange("p (h t j) -> p h t j", t=PACK, j=HALF)[:, h0:h1, t, :]
             acc = first[w, b, t][:, j0:j1].rearrange("p (h j) -> p h j", j=HALF)
             slp = nd[b, t][:, j0:j1].rearrange("p (h j) -> p h j", j=HALF)
             nc.vector.scalar_tensor_tensor(dst, acc, -1.0 if w == "b" else 1.0, slp, MULT, MULT)
 
-        def slope_step(b, t, *between):
-            gather_rows(b, t, 0, S)
-            for key in between:
-                weigh(*key, 0, S)
-            slope(b, t, 0, S)
+        def weigh_aside(w, b, t):
+            if (w, b) not in apart:
+                apart[w, b] = kept("apart%s%d" % (w, b), PACK * S, BF16, tag="apart" + w)
+            sums = kept("sums%d%d" % (b, t), S, F32, tag="sums%d" % t)
+            nc.scalar.copy(sums[:], first[w, b, t][:])
+            dst = apart[w, b][:].rearrange("p (h t j) -> p h t j", t=PACK, j=HALF)[:, :, t, :]
+            nc.gpsimd.tensor_tensor(
+                dst, sums[:].rearrange("p (h j) -> p h j", j=HALF), nd[b, t][:].rearrange("p (h j) -> p h j", j=HALF), MULT
+            )
 
         def weave(w, b, j0, j1, copy):
+            if (w, b) not in woven:
+                woven[w, b] = kept("woven%s%d" % (w, b), PACK * S, BF16, tag="wa_raw%d1" % "ba".index(w))
             cols = slice(PACK * j0, PACK * j1)
             copy(
                 woven[w, b][:, cols].rearrange("p (h c i t) -> p h c t i", t=PACK, i=RUN, c=HALF // RUN),
@@ -219,7 +220,7 @@ def tile_list_slope_weighted_commutator_kernel(
         banks = ["bank%s%d" % (w, t) for t in range(PACK) for w in "ba"]
         y = {}
 
-        def stage2(turn, b, t, j0, j1):
+        def stage2(turn, b, t, j0, j1, on_vector=False):
             acc = psum.tile([P, j1 - j0], F32, name="second", tag=banks[turn % len(banks)])
             passes = prods if j1 - j0 == HALF else prods[::-1]
             for n, (w, r) in enumerate(passes):
@@ -235,13 +236,17 @@ def tile_list_slope_weighted_commutator_kernel(
                 )
             y[b, t, j0] = res.tile([P, j1 - j0], F32, name="y", tag="y")
             c = b * PACK + t
-            nc.scalar.activation(y[b, t, j0][:], acc[:], COPY, scale=gain_t[:, c : c + 1])
+            if on_vector:
+                nc.vector.tensor_scalar(y[b, t, j0][:], acc[:], gain_t[:, c : c + 1], None, MULT)
+            else:
+                nc.scalar.activation(y[b, t, j0][:], acc[:], COPY, scale=gain_t[:, c : c + 1])
 
         def place(n, b, t, j0, j1):
+            part, c0 = (0, 0) if t == 0 else (1, (t - 1) * S)
             nc.vector.tensor_tensor(
                 windows[n % WINDOWS][:].indirect(idx2[:, j0 // 16 : j1 // 16]),
                 y[b, t, j0][:],
-                wgo_t[:, t * S + j0 : t * S + j1],
+                wgo_t[part][:, c0 + j0 : c0 + j1],
                 MULT,
             )
 
@@ -251,89 +256,94 @@ def tile_list_slope_weighted_commutator_kernel(
             )
 
         nc.sync.dma_start(idx[:], offs)
-        wb_raw_w = staged("wb_raw_w", I32)
-        load_wb(0)
-        load_table_scales()
-        load_wb(1)
-        load_table(0)
-        load_wb_scales()
-        load_table(1)
-        order_wb(0)
-        gather_table_scales()
-
-        load_rows(0, 0)
-        load_rows(0, 1)
         load_wa(0, 0)
-        load_rows(0, 2)
+        load_scales(tab_s, tab_scales)
         load_wa(1, 0)
+        load_scales(wb_raw_s, wb_scales)
+        load_table(0)
+        load_table(1)
+        load_rows(0, 0)
+        load_wb(0)
+        load_rows(0, 1)
+        load_rows(0, 2)
         load_rows(0, 3)
-        load_rows(1, 0)
         load_wa(0, 1)
-        load_rows(1, 1)
-
-        order_wb(1)
+        load_rows(1, 0)
         load_wa(1, 1)
-        gather_table(0)
+        load_wb(1)
+        load_rows(1, 1)
         load_rows(1, 2)
-        for a in range(PASSES):
-            order_wb_scales(a)
-        gather_table(1)
         load_rows(1, 3)
-        stage1("b", 0)
-
-        slope_step(0, 0)
-        wgo_t = staged("wgo_t", F32)
+        load_small()
         load_placing()
-        slope_step(0, 1, ("b", 0, 0))
+
+        def pick(b, t):
+            for j0 in (0, HALF):
+                gather_rows(b, t, j0, j0 + HALF)
+            for j0 in (0, HALF):
+                slope(b, t, j0, j0 + HALF)
+
+        def weigh_both(b, t):
+            for j0 in (0, HALF):
+                weigh("b", b, t, j0, j0 + HALF)
+            weigh_aside("a", b, t)
+
         cast_wa(0, 0)
-        slope_step(0, 2, ("b", 0, 1))
+        for a in range(PASSES):
+            gather_table_scales(a)
         quantise_wa(0, 0)
         cast_wa(1, 0)
-        slope_step(0, 3, ("b", 0, 2))
+        order_wb_scales()
+        gather_table(0)
         quantise_wa(1, 0)
+        gather_table(1)
         stage1("a", 0)
-        weigh("b", 0, 3, 0, S)
-        weave("b", 0, 0, S, nc.scalar.copy)
-
-        stage1("b", 1)
-        slope_step(1, 0, ("a", 0, 0))
+        pick(0, 0)
+        order_wb(0)
+        stage1("b", 0)
+        weigh_both(0, 0)
         for t in range(1, PACK):
-            weigh("a", 0, t, 0, S)
+            pick(0, t)
+            weigh_both(0, t)
         cast_wa(0, 1)
-        weave("a", 0, 0, S, nc.scalar.copy)
-        slope_step(1, 1, ("b", 1, 0))
-        quantise_h("b", 0, 0, S)
         quantise_wa(0, 1)
         cast_wa(1, 1)
-        slope_step(1, 2, ("b", 1, 1))
         quantise_wa(1, 1)
+        for w in "ba":
+            for j0 in (0, HALF):
+                weave(w, 0, j0, j0 + HALF, nc.scalar.copy)
+        pick(1, 0)
+        order_wb(1)
+        stage1("b", 1)
         stage1("a", 1)
+        quantise_h("b", 0, 0, S)
+        weigh_both(1, 0)
         quantise_h("a", 0, 0, S)
+        for t in range(1, PACK - 1):
+            pick(1, t)
+            weigh_both(1, t)
 
         last = PACK - 1
-        gather_rows(1, last, 0, HALF)
-        weigh("b", 1, last - 1, 0, S)
-        slope(1, last, 0, HALF)
-        gather_rows(1, last, HALF, S)
+        for j0 in (0, HALF):
+            gather_rows(1, last, j0, j0 + HALF)
+        for j0 in (0, HALF):
+            slope(1, last, j0, j0 + HALF)
         weigh("b", 1, last, 0, HALF)
         weave("b", 1, 0, HALF, nc.scalar.copy)
-        slope(1, last, HALF, S)
-        for t in range(last):
-            weigh("a", 1, t, 0, S)
         weigh("a", 1, last, 0, HALF)
         weigh("b", 1, last, HALF, S)
         weave("a", 1, 0, HALF, nc.vector.tensor_copy)
-        weave("b", 1, HALF, S, nc.scalar.copy)
+        weigh("a", 1, last, HALF, S)
         quantise_h("b", 1, 0, HALF)
         quantise_h("a", 1, 0, HALF)
-        weigh("a", 1, last, HALF, S)
-        weave("a", 1, HALF, S, nc.vector.tensor_copy)
+        weave("b", 1, HALF, S, nc.scalar.copy)
 
         outputs = [(b, t) for t in range(PACK) for b in range(PASSES)]
         for n in range(SPLIT):
-            stage2(n, *outputs[n], 0, HALF)
-        place(0, *outputs[0], 0, HALF)
+            stage2(n, *outputs[n], 0, HALF, on_vector=(n == 0))
+        weave("a", 1, HALF, S, nc.scalar.copy)
         quantise_h("b", 1, HALF, S)
+        place(0, *outputs[0], 0, HALF)
         quantise_h("a", 1, HALF, S)
         for n in range(1, SPLIT):
             place(n, *outputs[n], 0, HALF)

@@ -38,7 +38,7 @@ def tile_list_slope_weighted_commutator_kernel(
     with ExitStack() as ctx:
         keep = ctx.enter_context(tc.tile_pool(name="keep", bufs=1))
         cast = ctx.enter_context(tc.tile_pool(name="cast", bufs=2))
-        res = ctx.enter_context(tc.tile_pool(name="res", bufs=4))
+        res = ctx.enter_context(tc.tile_pool(name="res", bufs=3))
         psum = ctx.enter_context(tc.psum_pool(name="psum", bufs=1))
 
         def kept(name, width, dtype, tag=None):
@@ -46,9 +46,10 @@ def tile_list_slope_weighted_commutator_kernel(
 
         idx = keep.tile([P, S // 16], U16, name="idx")
         idx2 = keep.tile([P, S // 16], U16, name="idx2")
-        tab_s = kept("tab_s", PASSES * T, U8)
+        tab_s = kept("tab_s", T, U8)
+        v_rows = kept("v_rows", S, U8)
         v_w = [kept("v_w%d" % a, S, U32) for a in range(PASSES)]
-        v_s = [kept("v_s%d" % a, S, U8) for a in range(PASSES)]
+        v_s = kept("v_s", PASSES * S, U8)
         wb_raw_s = kept("wb_raw_s", PASSES * K, U8)
         wb_w = [kept("wb_w%d" % b, PASSES * SPAN, I32) for b in range(PASSES)]
         wb_s = kept("wb_s", PASSES * K, U8)
@@ -58,7 +59,7 @@ def tile_list_slope_weighted_commutator_kernel(
         slices = [(b, t) for b in range(PASSES) for t in range(PACK)]
         nd = {bt: kept("nd%d%d" % bt, S, F32) for bt in slices}
         prods = [(w, b) for b in range(PASSES) for w in "ba"]
-        h_w = {key: kept("h_w%s%d" % key, S, U32) for key in prods}
+        h_w = {}
         h_s = {key: kept("h_s%s%d" % key, S, U8) for key in prods}
         gain_t = kept("gain_t", PASSES * PACK, F32)
         wgo_t = [kept("wgo_first", S, F32), kept("wgo_rest", (PACK - 1) * S, F32)]
@@ -97,6 +98,11 @@ def tile_list_slope_weighted_commutator_kernel(
                     in_=scales.rearrange("a (q r) c -> r q a c", r=ROWS)[r].bitcast(I32),
                 )
 
+        def load_table_scales():
+            nc.sync.dma_start(
+                out=tab_s[0:P:PACK, :].bitcast(I32), in_=tab_scales.rearrange("a q c -> q a c").bitcast(I32)
+            )
+
         def load_table(a):
             tab_w[a] = kept("tab_w%d" % a, T, I32)
             nc.sync.dma_start(out=tab_w[a][:], in_=tab_words[a].rearrange("p c i -> p (c i)").bitcast(I32))
@@ -117,8 +123,13 @@ def tile_list_slope_weighted_commutator_kernel(
         def gather_table(a):
             nc.vector.tensor_copy(v_w[a][:], tab_w[a][:].bitcast(U32).indirect(idx[:]))
 
-        def gather_table_scales(a):
-            nc.vector.tensor_copy(v_s[a][:], tab_s[:, a * T : (a + 1) * T].indirect(idx[:]))
+        def gather_table_scales():
+            nc.vector.tensor_copy(v_rows[:], tab_s[:].indirect(idx[:]))
+            for q in range(QUADS):
+                nc.sync.dma_start(
+                    out=v_s[QUAD * q : QUAD * q + ROWS, :].bitcast(I32).rearrange("p (a c) -> p a c", a=PASSES),
+                    in_=v_rows[QUAD * q : QUAD * (q + 1) : PACK, :].bitcast(I32),
+                )
 
         def order_wb(b):
             nc.vector.tensor_copy(
@@ -156,9 +167,9 @@ def tile_list_slope_weighted_commutator_kernel(
         first = {}
 
         def stage1(ops, b):
-            for a in range(PASSES):
-                for t in range(PACK):
-                    for w in ops:
+            for t in range(PACK):
+                for w in ops:
+                    for a in range(PASSES):
                         if a == 0:
                             first[w, b, t] = psum.tile([P, S], F32, name="first", tag="bank%s%d" % (w, t))
                         codes, scales = weights(w, a, b, t)
@@ -167,7 +178,7 @@ def tile_list_slope_weighted_commutator_kernel(
                             lhsT=codes,
                             lhsT_scale=scales,
                             rhs=v_w[a][:].bitcast(E5M2),
-                            rhs_scale=v_s[a][:],
+                            rhs_scale=v_s[:, a * S : (a + 1) * S],
                             start=(a == 0),
                             stop=(a == PASSES - 1),
                         )
@@ -175,42 +186,50 @@ def tile_list_slope_weighted_commutator_kernel(
         picked, apart, woven = {}, {}, {}
 
         def gather_rows(b, t, j0, j1):
-            picked[b, t, j0] = res.tile([P, j1 - j0], F32, name="picked", tag="picked")
+            picked[b, t, j0] = res.tile([P, j1 - j0], F32, name="picked", tag="picked", bufs=4)
             nc.vector.tensor_copy(picked[b, t, j0][:], s_rows[b, t][:].indirect(idx[:, j0 // 16 : j1 // 16]))
 
         def slope(b, t, j0, j1):
             x = picked[b, t, j0][:]
             nc.vector.scalar_tensor_tensor(nd[b, t][:, j0:j1], x, 1.0, x, SUB, MULT)
 
-        def weigh(w, b, t, j0, j1):
+        def planes(w, b):
             if (w, b) not in apart:
-                apart[w, b] = kept("apart%s%d" % (w, b), PACK * S, BF16, tag="apart" + w)
-            h0, h1 = j0 // HALF, j1 // HALF
-            dst = apart[w, b][:].rearrange("p (h t j) -> p h t j", t=PACK, j=HALF)[:, h0:h1, t, :]
-            acc = first[w, b, t][:, j0:j1].rearrange("p (h j) -> p h j", j=HALF)
-            slp = nd[b, t][:, j0:j1].rearrange("p (h j) -> p h j", j=HALF)
-            nc.vector.scalar_tensor_tensor(dst, acc, -1.0 if w == "b" else 1.0, slp, MULT, MULT)
+                tag = "tab_w%d" % "ba".index(w) if b == 0 else ("wa_raw%d0" % "ba".index(w))
+                apart[w, b] = kept("apart%s%d" % (w, b), PACK * S, BF16 if w == "b" else F32, tag=tag)
+            return apart[w, b]
+
+        def weigh(w, b, t, j0, j1):
+            nc.vector.scalar_tensor_tensor(
+                planes(w, b)[:, t * S + j0 : t * S + j1],
+                first[w, b, t][:, j0:j1],
+                -1.0 if w == "b" else 1.0,
+                nd[b, t][:, j0:j1],
+                MULT,
+                MULT,
+            )
+
+        sums = {}
+
+        def park(w, b, t):
+            sums[b, t] = kept("sums%d%d" % (b, t), S, F32)
+            nc.scalar.copy(sums[b, t][:], first[w, b, t][:])
 
         def weigh_aside(w, b, t):
-            if (w, b) not in apart:
-                apart[w, b] = kept("apart%s%d" % (w, b), PACK * S, BF16, tag="apart" + w)
-            sums = kept("sums%d%d" % (b, t), S, F32, tag="sums%d" % t)
-            nc.scalar.copy(sums[:], first[w, b, t][:])
-            dst = apart[w, b][:].rearrange("p (h t j) -> p h t j", t=PACK, j=HALF)[:, :, t, :]
-            nc.gpsimd.tensor_tensor(
-                dst, sums[:].rearrange("p (h j) -> p h j", j=HALF), nd[b, t][:].rearrange("p (h j) -> p h j", j=HALF), MULT
-            )
+            nc.gpsimd.tensor_tensor(planes(w, b)[:, t * S : (t + 1) * S], sums[b, t][:], nd[b, t][:], MULT)
 
         def weave(w, b, j0, j1, copy):
             if (w, b) not in woven:
-                woven[w, b] = kept("woven%s%d" % (w, b), PACK * S, BF16, tag="wa_raw%d1" % "ba".index(w))
+                woven[w, b] = kept("woven%s%d" % (w, b), PACK * S, BF16, tag=WOVEN[w])
             cols = slice(PACK * j0, PACK * j1)
             copy(
-                woven[w, b][:, cols].rearrange("p (h c i t) -> p h c t i", t=PACK, i=RUN, c=HALF // RUN),
-                apart[w, b][:, cols].rearrange("p (h t c i) -> p h c t i", t=PACK, i=RUN, c=HALF // RUN),
+                woven[w, b][:, cols].rearrange("p (c i t) -> p c t i", t=PACK, i=RUN),
+                apart[w, b][:].rearrange("p (t c i) -> p c t i", t=PACK, i=RUN)[:, j0 // RUN : j1 // RUN],
             )
 
-        def quantise_h(w, b, j0, j1):
+        def quantise_h(w, b, j0, j1, tag=None):
+            if j0 == 0:
+                h_w[w, b] = kept("h_w%s%d" % (w, b), S, U32, tag=tag)
             nc.vector.quantize_mx(
                 out=h_w[w, b][:, j0:j1].bitcast(E4M3),
                 scales=h_s[w, b][:, j0:j1],
@@ -222,7 +241,9 @@ def tile_list_slope_weighted_commutator_kernel(
 
         def stage2(turn, b, t, j0, j1, on_vector=False):
             acc = psum.tile([P, j1 - j0], F32, name="second", tag=banks[turn % len(banks)])
-            passes = prods if j1 - j0 == HALF else prods[::-1]
+            passes = prods[::-1]
+            if j1 - j0 == HALF:
+                passes = prods if turn == 0 else prods[:2] + prods[:1:-1]
             for n, (w, r) in enumerate(passes):
                 codes, scales = weights("a" if w == "b" else "b", r, b, t)
                 nc.tensor.matmul_mx(
@@ -257,11 +278,12 @@ def tile_list_slope_weighted_commutator_kernel(
 
         nc.sync.dma_start(idx[:], offs)
         load_wa(0, 0)
-        load_scales(tab_s, tab_scales)
+        load_table_scales()
         load_wa(1, 0)
         load_scales(wb_raw_s, wb_scales)
         load_table(0)
         load_table(1)
+        gather_table_scales()
         load_rows(0, 0)
         load_wb(0)
         load_rows(0, 1)
@@ -277,20 +299,20 @@ def tile_list_slope_weighted_commutator_kernel(
         load_small()
         load_placing()
 
-        def pick(b, t):
+        WOVEN = {"b": "wa_raw01", "a": "wa_raw11"}
+
+        def gather_halves(b, t):
             for j0 in (0, HALF):
                 gather_rows(b, t, j0, j0 + HALF)
+
+        def weigh_slice(b, t):
             for j0 in (0, HALF):
                 slope(b, t, j0, j0 + HALF)
-
-        def weigh_both(b, t):
+            weigh_aside("a", b, t)
             for j0 in (0, HALF):
                 weigh("b", b, t, j0, j0 + HALF)
-            weigh_aside("a", b, t)
 
         cast_wa(0, 0)
-        for a in range(PASSES):
-            gather_table_scales(a)
         quantise_wa(0, 0)
         cast_wa(1, 0)
         order_wb_scales()
@@ -298,30 +320,33 @@ def tile_list_slope_weighted_commutator_kernel(
         quantise_wa(1, 0)
         gather_table(1)
         stage1("a", 0)
-        pick(0, 0)
+        for t in range(PACK):
+            park("a", 0, t)
         order_wb(0)
         stage1("b", 0)
-        weigh_both(0, 0)
-        for t in range(1, PACK):
-            pick(0, t)
-            weigh_both(0, t)
         cast_wa(0, 1)
         quantise_wa(0, 1)
         cast_wa(1, 1)
         quantise_wa(1, 1)
+        stage1("a", 1)
+        for t in range(PACK - 1):
+            park("a", 1, t)
+        order_wb(1)
+        for t in range(PACK):
+            gather_halves(0, t)
+            weigh_slice(0, t)
+        stage1("b", 1)
         for w in "ba":
             for j0 in (0, HALF):
                 weave(w, 0, j0, j0 + HALF, nc.scalar.copy)
-        pick(1, 0)
-        order_wb(1)
-        stage1("b", 1)
-        stage1("a", 1)
-        quantise_h("b", 0, 0, S)
-        weigh_both(1, 0)
-        quantise_h("a", 0, 0, S)
-        for t in range(1, PACK - 1):
-            pick(1, t)
-            weigh_both(1, t)
+        gather_halves(1, 0)
+        weigh_slice(1, 0)
+        gather_halves(1, 1)
+        quantise_h("b", 0, 0, S, tag=None)
+        weigh_slice(1, 1)
+        gather_halves(1, 2)
+        quantise_h("a", 0, 0, S, tag=None)
+        weigh_slice(1, 2)
 
         last = PACK - 1
         for j0 in (0, HALF):
@@ -340,12 +365,11 @@ def tile_list_slope_weighted_commutator_kernel(
 
         outputs = [(b, t) for t in range(PACK) for b in range(PASSES)]
         for n in range(SPLIT):
-            stage2(n, *outputs[n], 0, HALF, on_vector=(n == 0))
-        weave("a", 1, HALF, S, nc.scalar.copy)
+            stage2(n, *outputs[n], 0, HALF)
+        weave("a", 1, HALF, S, nc.vector.tensor_copy)
         quantise_h("b", 1, HALF, S)
-        place(0, *outputs[0], 0, HALF)
         quantise_h("a", 1, HALF, S)
-        for n in range(1, SPLIT):
+        for n in range(SPLIT):
             place(n, *outputs[n], 0, HALF)
         for n in range(len(outputs)):
             j0 = HALF if n < SPLIT else 0

@@ -50,7 +50,8 @@ def tile_list_slope_weighted_commutator_kernel(
         v_rows = kept("v_rows", S, U8)
         v_w = [kept("v_w%d" % a, S, U32) for a in range(PASSES)]
         v_s = kept("v_s", PASSES * S, U8)
-        wb_raw_s = kept("wb_raw_s", PASSES * K, U8)
+        wb_raw_s = kept("wb_raw_s", K, U8)
+        wb_rows = kept("wb_rows", K, U8)
         wb_w = [kept("wb_w%d" % b, PASSES * SPAN, I32) for b in range(PASSES)]
         wb_s = kept("wb_s", PASSES * K, U8)
         wa_parts = [(a, b) for b in range(PASSES) for a in range(PASSES)]
@@ -91,17 +92,17 @@ def tile_list_slope_weighted_commutator_kernel(
                 in_=wb_words[:, :, b * SPAN : (b + 1) * SPAN, :].rearrange("a p c i -> p a (c i)").bitcast(I32),
             )
 
-        def load_scales(plane, scales):
-            for r in range(ROWS):
-                nc.sync.dma_start(
-                    out=plane[r:P:QUAD, :].bitcast(I32).rearrange("p (a c) -> p a c", a=PASSES),
-                    in_=scales.rearrange("a (q r) c -> r q a c", r=ROWS)[r].bitcast(I32),
-                )
-
-        def load_table_scales():
+        def load_scales(rows, scales):
             nc.sync.dma_start(
-                out=tab_s[0:P:PACK, :].bitcast(I32), in_=tab_scales.rearrange("a q c -> q a c").bitcast(I32)
+                out=rows[0:P:PACK, :].bitcast(I32), in_=scales.rearrange("a q c -> q a c").bitcast(I32)
             )
+
+        def lower_scales(planes, rows):
+            for q in range(QUADS):
+                nc.sync.dma_start(
+                    out=planes[QUAD * q : QUAD * q + ROWS, :].bitcast(I32).rearrange("p (a c) -> p a c", a=PASSES),
+                    in_=rows[QUAD * q : QUAD * (q + 1) : PACK, :].bitcast(I32),
+                )
 
         def load_table(a):
             tab_w[a] = kept("tab_w%d" % a, T, I32)
@@ -125,11 +126,7 @@ def tile_list_slope_weighted_commutator_kernel(
 
         def gather_table_scales():
             nc.vector.tensor_copy(v_rows[:], tab_s[:].indirect(idx[:]))
-            for q in range(QUADS):
-                nc.sync.dma_start(
-                    out=v_s[QUAD * q : QUAD * q + ROWS, :].bitcast(I32).rearrange("p (a c) -> p a c", a=PASSES),
-                    in_=v_rows[QUAD * q : QUAD * (q + 1) : PACK, :].bitcast(I32),
-                )
+            lower_scales(v_s, v_rows)
 
         def order_wb(b):
             nc.vector.tensor_copy(
@@ -139,9 +136,10 @@ def tile_list_slope_weighted_commutator_kernel(
 
         def order_wb_scales():
             nc.vector.tensor_copy(
-                wb_s[:].rearrange("p (g t m) -> p g t m", t=PACK, m=P),
+                wb_rows[:].rearrange("p (g t m) -> p g t m", t=PACK, m=P),
                 wb_raw_s[:].rearrange("p (g m t) -> p g t m", t=PACK, m=P),
             )
+            lower_scales(wb_s, wb_rows)
 
         wa_bf = {}
 
@@ -276,9 +274,9 @@ def tile_list_slope_weighted_commutator_kernel(
                 out=out.rearrange("(b p t) c -> b t p c", p=P, t=PACK)[b, t], in_=windows[n % WINDOWS][:]
             )
 
-        nc.sync.dma_start(idx[:], offs)
         load_wa(0, 0)
-        load_table_scales()
+        nc.sync.dma_start(idx[:], offs)
+        load_scales(tab_s, tab_scales)
         load_wa(1, 0)
         load_scales(wb_raw_s, wb_scales)
         load_table(0)
@@ -286,6 +284,7 @@ def tile_list_slope_weighted_commutator_kernel(
         gather_table_scales()
         load_rows(0, 0)
         load_wb(0)
+        order_wb_scales()
         load_rows(0, 1)
         load_rows(0, 2)
         load_rows(0, 3)
@@ -315,7 +314,6 @@ def tile_list_slope_weighted_commutator_kernel(
         cast_wa(0, 0)
         quantise_wa(0, 0)
         cast_wa(1, 0)
-        order_wb_scales()
         gather_table(0)
         quantise_wa(1, 0)
         gather_table(1)

@@ -216,6 +216,12 @@ def tile_list_slope_weighted_commutator_kernel(
         def weigh_aside(w, b, t):
             nc.gpsimd.tensor_tensor(planes(w, b)[:, t * S : (t + 1) * S], sums[b, t][:], nd[b, t][:], MULT)
 
+        def weigh_woven(w, b, t):
+            if (w, b) not in woven:
+                woven[w, b] = kept("woven%s%d" % (w, b), PACK * S, BF16)
+            dst = woven[w, b][:].rearrange("p (j t) -> p t j", t=PACK)[:, t, :]
+            nc.gpsimd.tensor_tensor(dst, sums[b, t][:], nd[b, t][:], MULT)
+
         def weave(w, b, j0, j1, copy):
             if (w, b) not in woven:
                 woven[w, b] = kept("woven%s%d" % (w, b), PACK * S, BF16, tag=WOVEN[w])
@@ -307,7 +313,7 @@ def tile_list_slope_weighted_commutator_kernel(
         def weigh_slice(b, t):
             for j0 in (0, HALF):
                 slope(b, t, j0, j0 + HALF)
-            weigh_aside("a", b, t)
+            (weigh_woven if b == 0 else weigh_aside)("a", b, t)
             for j0 in (0, HALF):
                 weigh("b", b, t, j0, j0 + HALF)
 
@@ -334,16 +340,15 @@ def tile_list_slope_weighted_commutator_kernel(
             gather_halves(0, t)
             weigh_slice(0, t)
         stage1("b", 1)
-        for w in "ba":
-            for j0 in (0, HALF):
-                weave(w, 0, j0, j0 + HALF, nc.scalar.copy)
+        for j0 in (0, HALF):
+            weave("b", 0, j0, j0 + HALF, nc.scalar.copy)
+        quantise_h("a", 0, 0, S)
         gather_halves(1, 0)
         weigh_slice(1, 0)
         gather_halves(1, 1)
         quantise_h("b", 0, 0, S, tag=None)
         weigh_slice(1, 1)
         gather_halves(1, 2)
-        quantise_h("a", 0, 0, S, tag=None)
         weigh_slice(1, 2)
 
         last = PACK - 1

@@ -222,13 +222,13 @@ def tile_list_slope_weighted_commutator_kernel(
             dst = woven[w, b][:].rearrange("p (j t) -> p t j", t=PACK)[:, t, :]
             nc.gpsimd.tensor_tensor(dst, sums[b, t][:], nd[b, t][:], MULT)
 
-        def weave(w, b, j0, j1, copy):
+        def weave(w, b, j0, j1, copy, t0=0, t1=PACK):
             if (w, b) not in woven:
                 woven[w, b] = kept("woven%s%d" % (w, b), PACK * S, BF16, tag=WOVEN[w])
             cols = slice(PACK * j0, PACK * j1)
             copy(
-                woven[w, b][:, cols].rearrange("p (c i t) -> p c t i", t=PACK, i=RUN),
-                apart[w, b][:].rearrange("p (t c i) -> p c t i", t=PACK, i=RUN)[:, j0 // RUN : j1 // RUN],
+                woven[w, b][:, cols].rearrange("p (c i t) -> p c t i", t=PACK, i=RUN)[:, :, t0:t1],
+                apart[w, b][:].rearrange("p (t c i) -> p c t i", t=PACK, i=RUN)[:, j0 // RUN : j1 // RUN, t0:t1],
             )
 
         def quantise_h(w, b, j0, j1, tag=None):
@@ -348,6 +348,8 @@ def tile_list_slope_weighted_commutator_kernel(
         gather_halves(1, 1)
         quantise_h("b", 0, 0, S, tag=None)
         weigh_slice(1, 1)
+        for w in "ba":
+            weave(w, 1, 0, S, nc.scalar.copy, 0, 2)
         gather_halves(1, 2)
         weigh_slice(1, 2)
 
@@ -357,19 +359,19 @@ def tile_list_slope_weighted_commutator_kernel(
         for j0 in (0, HALF):
             slope(1, last, j0, j0 + HALF)
         weigh("b", 1, last, 0, HALF)
-        weave("b", 1, 0, HALF, nc.scalar.copy)
+        weave("b", 1, 0, HALF, nc.scalar.copy, 2, 4)
         weigh("a", 1, last, 0, HALF)
         weigh("b", 1, last, HALF, S)
-        weave("a", 1, 0, HALF, nc.vector.tensor_copy)
+        weave("a", 1, 0, HALF, nc.vector.tensor_copy, 2, 4)
         weigh("a", 1, last, HALF, S)
         quantise_h("b", 1, 0, HALF)
         quantise_h("a", 1, 0, HALF)
-        weave("b", 1, HALF, S, nc.scalar.copy)
+        weave("b", 1, HALF, S, nc.scalar.copy, 2, 4)
 
         outputs = [(b, t) for t in range(PACK) for b in range(PASSES)]
         for n in range(SPLIT):
             stage2(n, *outputs[n], 0, HALF)
-        weave("a", 1, HALF, S, nc.vector.tensor_copy)
+        weave("a", 1, HALF, S, nc.vector.tensor_copy, 2, 4)
         quantise_h("b", 1, HALF, S)
         quantise_h("a", 1, HALF, S)
         for n in range(SPLIT):

@@ -143,16 +143,22 @@ def tile_list_slope_weighted_commutator_kernel(
 
         wa_bf = {}
 
-        def cast_wa(a, b):
-            wa_bf[a, b] = cast.tile([P, PACK * SPAN], BF16, name="wa_bf", align_bytes=64)
+        def cast_wa(a, b, t0=0, t1=PACK):
+            if t0 == 0:
+                wa_bf[a, b] = cast.tile([P, PACK * SPAN], BF16, name="wa_bf", align_bytes=64)
             nc.scalar.activation(
-                wa_bf[a, b][:].rearrange("p (t m i) -> p m i t", t=PACK, i=PACK),
-                wa_raw[a, b][:].rearrange("p (i m t) -> p m i t", t=PACK, i=PACK),
+                wa_bf[a, b][:].rearrange("p (t m i) -> p m i t", t=PACK, i=PACK)[:, :, :, t0:t1],
+                wa_raw[a, b][:].rearrange("p (i m t) -> p m i t", t=PACK, i=PACK)[:, :, :, t0:t1],
                 COPY,
             )
 
-        def quantise_wa(a, b):
-            nc.vector.quantize_mx(out=wa_w[a, b][:].bitcast(E4M3), scales=wa_s[a, b][:], in_=wa_bf[a, b][:])
+        def quantise_wa(a, b, t0=0, t1=PACK):
+            cols = slice(t0 * P, t1 * P)
+            nc.vector.quantize_mx(
+                out=wa_w[a, b][:, cols].bitcast(E4M3),
+                scales=wa_s[a, b][:, cols],
+                in_=wa_bf[a, b][:, t0 * SPAN : t1 * SPAN],
+            )
 
         def weights(w, a, b, t):
             if w == "a":
@@ -193,7 +199,7 @@ def tile_list_slope_weighted_commutator_kernel(
 
         def planes(w, b):
             if (w, b) not in apart:
-                tag = "tab_w%d" % "ba".index(w) if b == 0 else ("wa_raw%d0" % "ba".index(w))
+                tag = "tab_w%d" % "ba".index(w) if b == 0 else ("s_rows11", "wa_raw10")["ba".index(w)]
                 apart[w, b] = kept("apart%s%d" % (w, b), PACK * S, BF16 if w == "b" else F32, tag=tag)
             return apart[w, b]
 
@@ -330,8 +336,9 @@ def tile_list_slope_weighted_commutator_kernel(
         stage1("b", 0)
         cast_wa(0, 1)
         quantise_wa(0, 1)
-        cast_wa(1, 1)
-        quantise_wa(1, 1)
+        for t0 in (0, 2):
+            cast_wa(1, 1, t0, t0 + 2)
+            quantise_wa(1, 1, t0, t0 + 2)
         stage1("a", 1)
         for t in range(PACK - 1):
             park("a", 1, t)

@@ -128,10 +128,10 @@ def tile_list_slope_weighted_commutator_kernel(
             nc.vector.tensor_copy(v_rows[:], tab_s[:].indirect(idx[:]))
             lower_scales(v_s, v_rows)
 
-        def order_wb(b):
+        def order_wb(b, t0=0, t1=PACK):
             nc.vector.tensor_copy(
-                wb_w[b][:].rearrange("p (a t c i) -> p a c t i", t=PACK, i=RUN, c=P // RUN),
-                wb_raw_w[b][:].rearrange("p (a c i t) -> p a c t i", t=PACK, i=RUN, c=P // RUN),
+                wb_w[b][:].rearrange("p (a t c i) -> p a c t i", t=PACK, i=RUN, c=P // RUN)[:, :, :, t0:t1],
+                wb_raw_w[b][:].rearrange("p (a c i t) -> p a c t i", t=PACK, i=RUN, c=P // RUN)[:, :, :, t0:t1],
             )
 
         def order_wb_scales():
@@ -170,10 +170,10 @@ def tile_list_slope_weighted_commutator_kernel(
 
         first = {}
 
-        def stage1(ops, b):
+        def stage1(steps, b):
             for t in range(PACK):
-                for w in ops:
-                    for a in range(PASSES):
+                for w, passes in steps:
+                    for a in passes:
                         if a == 0:
                             first[w, b, t] = psum.tile([P, S], F32, name="first", tag="bank%s%d" % (w, t))
                         codes, scales = weights(w, a, b, t)
@@ -199,7 +199,7 @@ def tile_list_slope_weighted_commutator_kernel(
 
         def planes(w, b):
             if (w, b) not in apart:
-                tag = "tab_w%d" % "ba".index(w) if b == 0 else ("s_rows11", "wa_raw10")["ba".index(w)]
+                tag = "tab_w%d" % "ba".index(w) if b == 0 else ("tab_w1", "wa_raw10")["ba".index(w)]
                 apart[w, b] = kept("apart%s%d" % (w, b), PACK * S, BF16 if w == "b" else F32, tag=tag)
             return apart[w, b]
 
@@ -292,12 +292,12 @@ def tile_list_slope_weighted_commutator_kernel(
         load_wa(1, 0)
         load_scales(wb_raw_s, wb_scales)
         load_table(0)
+        load_rows(0, 0)
         load_table(1)
         gather_table_scales()
-        load_rows(0, 0)
         load_wb(0)
-        order_wb_scales()
         load_rows(0, 1)
+        order_wb_scales()
         load_rows(0, 2)
         load_rows(0, 3)
         load_wa(0, 1)
@@ -329,31 +329,32 @@ def tile_list_slope_weighted_commutator_kernel(
         gather_table(0)
         quantise_wa(1, 0)
         gather_table(1)
-        stage1("a", 0)
+        stage1([("a", (0, 1))], 0)
         for t in range(PACK):
             park("a", 0, t)
         order_wb(0)
-        stage1("b", 0)
+        stage1([("b", (0, 1))], 0)
         cast_wa(0, 1)
         quantise_wa(0, 1)
+        stage1([("a", (0,))], 1)
         for t0 in (0, 2):
             cast_wa(1, 1, t0, t0 + 2)
             quantise_wa(1, 1, t0, t0 + 2)
-        stage1("a", 1)
-        for t in range(PACK - 1):
-            park("a", 1, t)
-        order_wb(1)
+        for t0 in (0, 2):
+            order_wb(1, t0, t0 + 2)
         for t in range(PACK):
             gather_halves(0, t)
             weigh_slice(0, t)
-        stage1("b", 1)
+        stage1([("b", (0, 1)), ("a", (1,))], 1)
+        for t in range(PACK - 1):
+            park("a", 1, t)
         for j0 in (0, HALF):
             weave("b", 0, j0, j0 + HALF, nc.scalar.copy)
-        quantise_h("a", 0, 0, S)
         gather_halves(1, 0)
+        quantise_h("a", 0, 0, S, tag="s_rows10")
+        quantise_h("b", 0, 0, S)
         weigh_slice(1, 0)
         gather_halves(1, 1)
-        quantise_h("b", 0, 0, S, tag=None)
         weigh_slice(1, 1)
         for w in "ba":
             weave(w, 1, 0, S, nc.scalar.copy, 0, 2)

@@ -28,6 +28,7 @@ LIVE = (QUADS - 1) * QUAD + ROWS
 RUN = 4
 HALF = S // 2
 WINDOWS = 3
+LEAD = S // 4
 SPLIT = 2
 
 
@@ -252,7 +253,7 @@ def tile_list_slope_weighted_commutator_kernel(
         def stage2(turn, b, t, j0, j1, on_vector=False):
             acc = psum.tile([P, j1 - j0], F32, name="second", tag=banks[turn % len(banks)])
             passes = prods[::-1]
-            if j1 - j0 == HALF:
+            if j1 - j0 < S:
                 passes = prods if turn == 0 else prods[:2] + prods[:1:-1]
             for n, (w, r) in enumerate(passes):
                 codes, scales = weights("a" if w == "b" else "b", r, b, t)
@@ -265,7 +266,7 @@ def tile_list_slope_weighted_commutator_kernel(
                     start=(n == 0),
                     stop=(n == len(prods) - 1),
                 )
-            y[b, t, j0] = res.tile([P, j1 - j0], F32, name="y", tag="y")
+            y[b, t, j0] = res.tile([P, j1 - j0], F32, name="y", tag="y", bufs=4)
             c = b * PACK + t
             if on_vector:
                 nc.vector.tensor_scalar(y[b, t, j0][:], acc[:], gain_t[:, c : c + 1], None, MULT)
@@ -377,15 +378,17 @@ def tile_list_slope_weighted_commutator_kernel(
         weave("b", 1, HALF, S, nc.scalar.copy, 2, 4)
 
         outputs = [(b, t) for t in range(PACK) for b in range(PASSES)]
-        for n in range(SPLIT):
-            stage2(n, *outputs[n], 0, HALF)
-        weave("a", 1, HALF, S, nc.vector.tensor_copy, 2, 4)
+        early = [(0, 0, LEAD), (1, 0, HALF), (0, LEAD, HALF)]
+        weave("a", 1, S - LEAD, S, nc.scalar.copy, 2, 4)
+        for turn, (n, j0, j1) in enumerate(early):
+            stage2(turn, *outputs[n], j0, j1)
+        weave("a", 1, HALF, S - LEAD, nc.vector.tensor_copy, 2, 4)
         quantise_h("b", 1, HALF, S)
         quantise_h("a", 1, HALF, S)
-        for n in range(SPLIT):
-            place(n, *outputs[n], 0, HALF)
-        for n in range(len(outputs)):
+        for n, j0, j1 in early:
+            place(n, *outputs[n], j0, j1)
+        for turn, n in enumerate([1, 0] + list(range(SPLIT, len(outputs)))):
             j0 = HALF if n < SPLIT else 0
-            stage2(SPLIT + n, *outputs[n], j0, S)
+            stage2(len(early) + turn, *outputs[n], j0, S)
             place(n, *outputs[n], j0, S)
             store(n, *outputs[n])

@@ -293,9 +293,9 @@ def tile_list_slope_weighted_commutator_kernel(
         load_wa(1, 0)
         load_scales(wb_raw_s, wb_scales)
         load_table(0)
+        gather_table_scales()
         load_rows(0, 0)
         load_table(1)
-        gather_table_scales()
         load_wb(0)
         load_rows(0, 1)
         order_wb_scales()

@@ -191,11 +191,15 @@ def tile_list_slope_weighted_commutator_kernel(
         picked, apart, woven = {}, {}, {}
 
         def gather_rows(b, t, j0, j1):
-            picked[b, t, j0] = res.tile([P, j1 - j0], F32, name="picked", tag="picked", bufs=4)
-            nc.vector.tensor_copy(picked[b, t, j0][:], s_rows[b, t][:].indirect(idx[:, j0 // 16 : j1 // 16]))
+            if (b, t, j0) == (1, 1, 0):
+                picked[b, t, j0] = planes("a", 1)[:, 0:HALF]
+            else:
+                tile = res.tile([P, j1 - j0], F32, name="picked", tag="picked", bufs=4)
+                picked[b, t, j0] = tile[:]
+            nc.vector.tensor_copy(picked[b, t, j0], s_rows[b, t][:].indirect(idx[:, j0 // 16 : j1 // 16]))
 
         def slope(b, t, j0, j1):
-            x = picked[b, t, j0][:]
+            x = picked[b, t, j0]
             nc.vector.scalar_tensor_tensor(nd[b, t][:, j0:j1], x, 1.0, x, SUB, MULT)
 
         def planes(w, b):
@@ -347,16 +351,20 @@ def tile_list_slope_weighted_commutator_kernel(
             gather_halves(0, t)
             weigh_slice(0, t)
         stage1([("b", (0, 1)), ("a", (1,))], 1)
-        for t in range(PACK - 1):
+        for t in range(1, PACK - 1):
             park("a", 1, t)
         for j0 in (0, HALF):
             weave("b", 0, j0, j0 + HALF, nc.scalar.copy)
         gather_halves(1, 0)
         quantise_h("a", 0, 0, S, tag="s_rows10")
         quantise_h("b", 0, 0, S)
-        weigh_slice(1, 0)
+        for j0 in (0, HALF):
+            slope(1, 0, j0, j0 + HALF)
+        for j0 in (0, HALF):
+            weigh("b", 1, 0, j0, j0 + HALF)
         gather_halves(1, 1)
         weigh_slice(1, 1)
+        weigh("a", 1, 0, 0, S)
         for w in "ba":
             weave(w, 1, 0, S, nc.scalar.copy, 0, 2)
         gather_halves(1, 2)

from contextlib import ExitStack

import concourse.mybir as mybir

K, T, S, T2 = 1024, 2048, 512, 1024
FLOPS = 4 * 2 * K * K * S

F32 = mybir.dt.float32
BF16 = mybir.dt.bfloat16
I32 = mybir.dt.int32
U32 = mybir.dt.uint32
U16 = mybir.dt.uint16
U8 = mybir.dt.uint8
E4M3 = mybir.dt.float8_e4m3fn_x4
E5M2 = mybir.dt.float8_e5m2_x4
MULT = mybir.AluOpType.mult
SUB = mybir.AluOpType.subtract
COPY = mybir.ActivationFunctionType.Copy

P = 128
PACK = 4
SPAN = P * PACK
PASSES = K // SPAN
QUADS = 4
QUAD = P // QUADS
ROWS = 4
LIVE = (QUADS - 1) * QUAD + ROWS
RUN = 4
HALF = S // 2
WINDOWS = 3
LEAD = S // 4
SPLIT = 2


def tile_list_slope_weighted_commutator_kernel(
    tc, tab_words, tab_scales, wa, wb_words, wb_scales, sT, gain, wgo, offs, offs2, out
):
    nc = tc.nc
    with ExitStack() as ctx:
        keep = ctx.enter_context(tc.tile_pool(name="keep", bufs=1))
        cast = ctx.enter_context(tc.tile_pool(name="cast", bufs=2))
        res = ctx.enter_context(tc.tile_pool(name="res", bufs=3))
        psum = ctx.enter_context(tc.psum_pool(name="psum", bufs=1))

        def kept(name, width, dtype, tag=None):
            return keep.tile([P, width], dtype, name=name, tag=tag or name, align_bytes=64)

        idx = keep.tile([P, S // 16], U16, name="idx")
        idx2 = keep.tile([P, S // 16], U16, name="idx2")
        tab_s = kept("tab_s", T, U8)
        v_rows = kept("v_rows", S, U8)
        v_w = [kept("v_w%d" % a, S, U32) for a in range(PASSES)]
        v_s = kept("v_s", PASSES * S, U8)
        wb_raw_s = kept("wb_raw_s", K, U8)
        wb_rows = kept("wb_rows", K, U8)
        wb_w = [kept("wb_w%d" % b, PASSES * SPAN, I32) for b in range(PASSES)]
        wb_s = kept("wb_s", PASSES * K, U8)
        wa_parts = [(a, b) for b in range(PASSES) for a in range(PASSES)]
        wa_w = {ab: kept("wa_w%d%d" % ab, SPAN, U32) for ab in wa_parts}
        wa_s = {ab: kept("wa_s%d%d" % ab, SPAN, U8) for ab in wa_parts}
        slices = [(b, t) for b in range(PASSES) for t in range(PACK)]
        nd = {bt: kept("nd%d%d" % bt, S, F32) for bt in slices}
        prods = [(w, b) for b in range(PASSES) for w in "ba"]
        h_w = {}
        h_s = {key: kept("h_s%s%d" % key, S, U8) for key in prods}
        gain_t = kept("gain_t", PASSES * PACK, F32)
        wgo_t = [kept("wgo_first", S, F32), kept("wgo_rest", (PACK - 1) * S, F32)]
        windows = [kept("window%d" % i, T2, F32) for i in range(WINDOWS)]

        nc.gpsimd.memset(tab_s[:].bitcast(I32), 0)
        nc.vector.memset(wb_raw_s[:].bitcast(I32), 0)
        for window in windows:
            nc.vector.memset(window[:], 0.0)

        s_rows, wa_raw, tab_w, wb_raw_w = {}, {}, {}, {}

        def load_rows(b, t):
            s_rows[b, t] = kept("s_rows%d%d" % (b, t), T, F32)
            nc.sync.dma_start(out=s_rows[b, t][:], in_=sT.rearrange("(b p t) c -> b t p c", p=P, t=PACK)[b, t])

        def load_wa(a, b, i0=0, i1=PACK):
            if i0 == 0:
                wa_raw[a, b] = kept("wa_raw%d%d" % (a, b), PACK * SPAN, F32)
            rows = wa[a * SPAN : (a + 1) * SPAN, b * SPAN : (b + 1) * SPAN].rearrange("(p i) c -> p i c", i=PACK)
            nc.sync.dma_start(
                out=wa_raw[a, b][:, i0 * SPAN : i1 * SPAN].rearrange("p (i c) -> p i c", c=SPAN), in_=rows[:, i0:i1, :]
            )

        def load_wb(b):
            wb_raw_w[b] = kept("wb_raw_w%d" % b, PASSES * SPAN, I32)
            nc.sync.dma_start(
                out=wb_raw_w[b][:].rearrange("p (a c) -> p a c", a=PASSES),
                in_=wb_words[:, :, b * SPAN : (b + 1) * SPAN, :].rearrange("a p c i -> p a (c i)").bitcast(I32),
            )

        def load_scales(rows, scales):
            nc.sync.dma_start(
                out=rows[0:P:PACK, :].bitcast(I32), in_=scales.rearrange("a q c -> q a c").bitcast(I32)
            )

        def lower_scales(planes, rows):
            for q in range(QUADS):
                nc.sync.dma_start(
                    out=planes[QUAD * q : QUAD * q + ROWS, :].bitcast(I32).rearrange("p (a c) -> p a c", a=PASSES),
                    in_=rows[QUAD * q : QUAD * (q + 1) : PACK, :].bitcast(I32),
                )

        def load_table(a):
            tab_w[a] = kept("tab_w%d" % a, T, I32)
            nc.sync.dma_start(out=tab_w[a][:], in_=tab_words[a].rearrange("p c i -> p (c i)").bitcast(I32))

        def load_small():
            nc.sync.dma_start(idx2[:], offs2)
            nc.sync.dma_start(
                out=gain_t[:].rearrange("p (b t) -> p b t", t=PACK),
                in_=gain.rearrange("(b p t) -> p b t", p=P, t=PACK),
            )

        def load_placing():
            rows = wgo.rearrange("(p t) j -> p (t j)", t=PACK)
            for part, cols in enumerate((slice(0, S), slice(S, PACK * S))):
                for q in range(QUADS):
                    nc.sync.dma_start(out=wgo_t[part][QUAD * q : QUAD * (q + 1), :], in_=rows[:, cols])

        def gather_table(a):
            nc.vector.tensor_copy(v_w[a][:], tab_w[a][:].bitcast(U32).indirect(idx[:]))

        def gather_table_scales():
            nc.vector.tensor_copy(v_rows[:], tab_s[:].indirect(idx[:]))
            lower_scales(v_s, v_rows)

        def order_wb(b, t0=0, t1=PACK):
            nc.vector.tensor_copy(
                wb_w[b][:].rearrange("p (a t c i) -> p a c t i", t=PACK, i=RUN, c=P // RUN)[:, :, :, t0:t1],
                wb_raw_w[b][:].rearrange("p (a c i t) -> p a c t i", t=PACK, i=RUN, c=P // RUN)[:, :, :, t0:t1],
            )

        def order_wb_scales():
            nc.vector.tensor_copy(
                wb_rows[:].rearrange("p (g t m) -> p g t m", t=PACK, m=P),
                wb_raw_s[:].rearrange("p (g m t) -> p g t m", t=PACK, m=P),
            )
            lower_scales(wb_s, wb_rows)

        wa_bf = {}

        def cast_wa(a, b, t0=0, t1=PACK):
            if t0 == 0:
                wa_bf[a, b] = cast.tile([P, PACK * SPAN], BF16, name="wa_bf", align_bytes=64)
            nc.scalar.activation(
                wa_bf[a, b][:].rearrange("p (t m i) -> p m i t", t=PACK, i=PACK)[:, :, :, t0:t1],
                wa_raw[a, b][:].rearrange("p (i m t) -> p m i t", t=PACK, i=PACK)[:, :, :, t0:t1],
                COPY,
            )

        def quantise_wa(a, b, t0=0, t1=PACK):
            cols = slice(t0 * P, t1 * P)
            nc.vector.quantize_mx(
                out=wa_w[a, b][:, cols].bitcast(E4M3),
                scales=wa_s[a, b][:, cols],
                in_=wa_bf[a, b][:, t0 * SPAN : t1 * SPAN],
            )

        def weights(w, a, b, t):
            if w == "a":
                cols = slice(t * P, (t + 1) * P)
                return wa_w[a, b][:, cols].bitcast(E4M3), wa_s[a, b][:, cols]
            c0 = a * SPAN + t * P
            s0 = a * K + b * SPAN + t * P
            return wb_w[b][:, c0 : c0 + P].bitcast(E4M3), wb_s[:, s0 : s0 + P]

        first = {}

        def stage1(steps, b):
            for t in range(PACK):
                for w, passes in steps:
                    for a in passes:
                        if a == 0:
                            first[w, b, t] = psum.tile([P, S], F32, name="first", tag="bank%s%d" % (w, t))
                        codes, scales = weights(w, a, b, t)
                        nc.tensor.matmul_mx(
                            out=first[w, b, t][:],
                            lhsT=codes,
                            lhsT_scale=scales,
                            rhs=v_w[a][:].bitcast(E5M2),
                            rhs_scale=v_s[:, a * S : (a + 1) * S],
                            start=(a == 0),
                            stop=(a == PASSES - 1),
                        )

        picked, apart, woven = {}, {}, {}

        def gather_rows(b, t, j0, j1):
            if (b, t, j0) == (1, 1, 0):
                picked[b, t, j0] = planes("a", 1)[:, 0:HALF]
            else:
                tile = res.tile([P, j1 - j0], F32, name="picked", tag="picked", bufs=4)
                picked[b, t, j0] = tile[:]
            nc.vector.tensor_copy(picked[b, t, j0], s_rows[b, t][:].indirect(idx[:, j0 // 16 : j1 // 16]))

        def slope(b, t, j0, j1):
            x = picked[b, t, j0]
            nc.vector.scalar_tensor_tensor(nd[b, t][:, j0:j1], x, 1.0, x, SUB, MULT)

        def planes(w, b):
            if (w, b) not in apart:
                tag = "tab_w%d" % "ba".index(w) if b == 0 else ("tab_w1", "wa_raw10")["ba".index(w)]
                apart[w, b] = kept("apart%s%d" % (w, b), PACK * S, BF16 if w == "b" else F32, tag=tag)
            return apart[w, b]

        def weigh(w, b, t, j0, j1):
            nc.vector.scalar_tensor_tensor(
                planes(w, b)[:, t * S + j0 : t * S + j1],
                first[w, b, t][:, j0:j1],
                -1.0 if w == "b" else 1.0,
                nd[b, t][:, j0:j1],
                MULT,
                MULT,
            )

        sums = {}

        def park(w, b, t):
            sums[b, t] = kept("sums%d%d" % (b, t), S, F32)
            nc.scalar.copy(sums[b, t][:], first[w, b, t][:])

        def weigh_aside(w, b, t):
            nc.gpsimd.tensor_tensor(planes(w, b)[:, t * S : (t + 1) * S], sums[b, t][:], nd[b, t][:], MULT)

        def weigh_woven(w, b, t):
            if (w, b) not in woven:
                woven[w, b] = kept("woven%s%d" % (w, b), PACK * S, BF16)
            dst = woven[w, b][:].rearrange("p (j t) -> p t j", t=PACK)[:, t, :]
            nc.gpsimd.tensor_tensor(dst, sums[b, t][:], nd[b, t][:], MULT)

        def weave(w, b, j0, j1, copy, t0=0, t1=PACK):
            if (w, b) not in woven:
                woven[w, b] = kept("woven%s%d" % (w, b), PACK * S, BF16, tag=WOVEN[w])
            cols = slice(PACK * j0, PACK * j1)
            copy(
                woven[w, b][:, cols].rearrange("p (c i t) -> p c t i", t=PACK, i=RUN)[:, :, t0:t1],
                apart[w, b][:].rearrange("p (t c i) -> p c t i", t=PACK, i=RUN)[:, j0 // RUN : j1 // RUN, t0:t1],
            )

        def quantise_h(w, b, j0, j1, tag=None):
            if j0 == 0:
                h_w[w, b] = kept("h_w%s%d" % (w, b), S, U32, tag=tag)
            nc.vector.quantize_mx(
                out=h_w[w, b][:, j0:j1].bitcast(E4M3),
                scales=h_s[w, b][:, j0:j1],
                in_=woven[w, b][:, PACK * j0 : PACK * j1],
            )

        banks = ["bank%s%d" % (w, t) for t in range(PACK) for w in "ba"]
        y = {}

        def stage2(turn, b, t, j0, j1, on_vector=False):
            acc = psum.tile([P, j1 - j0], F32, name="second", tag=banks[turn % len(banks)])
            passes = prods[::-1]
            if j1 - j0 < S:
                passes = prods if turn == 0 else prods[:2] + prods[:1:-1]
            for n, (w, r) in enumerate(passes):
                codes, scales = weights("a" if w == "b" else "b", r, b, t)
                nc.tensor.matmul_mx(
                    out=acc[:],
                    lhsT=codes,
                    lhsT_scale=scales,
                    rhs=h_w[w, r][:, j0:j1].bitcast(E4M3),
                    rhs_scale=h_s[w, r][:, j0:j1],
                    start=(n == 0),
                    stop=(n == len(prods) - 1),
                )
            y[b, t, j0] = res.tile([P, j1 - j0], F32, name="y", tag="y", bufs=4)
            c = b * PACK + t
            if on_vector:
                nc.vector.tensor_scalar(y[b, t, j0][:], acc[:], gain_t[:, c : c + 1], None, MULT)
            else:
                nc.scalar.activation(y[b, t, j0][:], acc[:], COPY, scale=gain_t[:, c : c + 1])

        def place(n, b, t, j0, j1):
            part, c0 = (0, 0) if t == 0 else (1, (t - 1) * S)
            nc.vector.tensor_tensor(
                windows[n % WINDOWS][:].indirect(idx2[:, j0 // 16 : j1 // 16]),
                y[b, t, j0][:],
                wgo_t[part][:, c0 + j0 : c0 + j1],
                MULT,
            )

        def store(n, b, t):
            nc.sync.dma_start(
                out=out.rearrange("(b p t) c -> b t p c", p=P, t=PACK)[b, t], in_=windows[n % WINDOWS][:]
            )

        load_wa(0, 0)
        nc.sync.dma_start(idx[:], offs)
        load_scales(tab_s, tab_scales)
        load_wa(1, 0)
        load_scales(wb_raw_s, wb_scales)
        load_table(0)
        gather_table_scales()
        load_rows(0, 0)
        load_table(1)
        load_wb(0)
        load_rows(0, 1)
        order_wb_scales()
        load_rows(0, 2)
        load_rows(0, 3)
        load_wa(0, 1)
        load_rows(1, 0)
        load_wa(1, 1)
        load_wb(1)
        load_rows(1, 1)
        load_rows(1, 2)
        load_rows(1, 3)
        load_small()
        load_placing()

        WOVEN = {"b": "wa_raw01", "a": "wa_raw11"}

        def gather_halves(b, t):
            for j0 in (0, HALF):
                gather_rows(b, t, j0, j0 + HALF)

        def weigh_slice(b, t):
            for j0 in (0, HALF):
                slope(b, t, j0, j0 + HALF)
            (weigh_woven if b == 0 else weigh_aside)("a", b, t)
            for j0 in (0, HALF):
                weigh("b", b, t, j0, j0 + HALF)

        cast_wa(0, 0)
        quantise_wa(0, 0)
        cast_wa(1, 0)
        gather_table(0)
        quantise_wa(1, 0)
        gather_table(1)
        stage1([("a", (0, 1))], 0)
        for t in range(PACK):
            park("a", 0, t)
        order_wb(0)
        stage1([("b", (0, 1))], 0)
        cast_wa(0, 1)
        quantise_wa(0, 1)
        stage1([("a", (0,))], 1)
        for t0 in (0, 2):
            cast_wa(1, 1, t0, t0 + 2)
            quantise_wa(1, 1, t0, t0 + 2)
        for t0 in (0, 2):
            order_wb(1, t0, t0 + 2)
        for t in range(PACK):
            gather_halves(0, t)
            weigh_slice(0, t)
        stage1([("b", (0, 1)), ("a", (1,))], 1)
        for t in range(1, PACK - 1):
            park("a", 1, t)
        for j0 in (0, HALF):
            weave("b", 0, j0, j0 + HALF, nc.scalar.copy)
        gather_halves(1, 0)
        quantise_h("a", 0, 0, S, tag="s_rows10")
        quantise_h("b", 0, 0, S)
        for j0 in (0, HALF):
            slope(1, 0, j0, j0 + HALF)
        for j0 in (0, HALF):
            weigh("b", 1, 0, j0, j0 + HALF)
        gather_halves(1, 1)
        weigh_slice(1, 1)
        weigh("a", 1, 0, 0, S)
        for w in "ba":
            weave(w, 1, 0, S, nc.scalar.copy, 0, 2)
        gather_halves(1, 2)
        weigh_slice(1, 2)

        last = PACK - 1
        for j0 in (0, HALF):
            gather_rows(1, last, j0, j0 + HALF)
        for j0 in (0, HALF):
            slope(1, last, j0, j0 + HALF)
        weigh("b", 1, last, 0, HALF)
        weave("b", 1, 0, HALF, nc.scalar.copy, 2, 4)
        weigh("a", 1, last, 0, HALF)
        weigh("b", 1, last, HALF, S)
        weave("a", 1, 0, HALF, nc.vector.tensor_copy, 2, 4)
        weigh("a", 1, last, HALF, S)
        quantise_h("b", 1, 0, HALF)
        quantise_h("a", 1, 0, HALF)
        weave("b", 1, HALF, S, nc.scalar.copy, 2, 4)

        outputs = [(b, t) for t in range(PACK) for b in range(PASSES)]
        early = [(0, 0, LEAD), (1, 0, HALF), (0, LEAD, HALF)]
        weave("a", 1, S - LEAD, S, nc.scalar.copy, 2, 4)
        for turn, (n, j0, j1) in enumerate(early):
            stage2(turn, *outputs[n], j0, j1)
        weave("a", 1, HALF, S - LEAD, nc.vector.tensor_copy, 2, 4)
        quantise_h("b", 1, HALF, S)
        quantise_h("a", 1, HALF, S)
        for n, j0, j1 in early:
            place(n, *outputs[n], j0, j1)
        for turn, n in enumerate([1, 0] + list(range(SPLIT, len(outputs)))):
            j0 = HALF if n < SPLIT else 0
            stage2(len(early) + turn, *outputs[n], j0, S)
            place(n, *outputs[n], j0, S)
            store(n, *outputs[n])
